import numpy as np
import ml_dtypes


def mxq(x, axis, fmt="e4m3"):
    dtype, down = {"e4m3": (ml_dtypes.float8_e4m3fn, 7), "e5m2": (ml_dtypes.float8_e5m2, 14)}[fmt]
    v = np.moveaxis(np.asarray(x, np.float32).astype(ml_dtypes.bfloat16).astype(np.float64), axis, -1)
    blocks = v.reshape(v.shape[:-1] + (-1, 32))
    amax = np.abs(blocks).max(-1, keepdims=True)
    byte = np.maximum(np.where(amax > 0, np.frexp(amax)[1] - 1 + 127, 0) - down, 1)
    scale = np.exp2(byte - 127.0)
    codes = (blocks / scale).astype(np.float32).astype(dtype).astype(np.float64)
    return np.moveaxis((codes * scale).reshape(v.shape), -1, axis)


WIDE = False


def mx_kscale(k):
    if not WIDE:
        return np.ones(k)
    levels = np.array([10, -10, 5, -5, 0])
    if k % 512:
        return np.exp2(np.random.permutation(np.resize(levels, k // 32))).repeat(32)
    a = np.empty((k // 512, 16))
    for p in range(k // 512):
        a[p, :8] = np.random.permutation(np.resize(levels, 8))
        for g in range(8):
            far = levels[np.abs(levels - a[p, g]) >= 10]
            a[p, g + 8] = far[np.random.randint(len(far))]
    return np.exp2(a.ravel()).repeat(32)


def f64(x):
    return np.asarray(x).astype(np.float64)


def striped(idx):
    return np.tile(idx.reshape(-1, 16).T, (8, 1)).astype(np.uint16)


def unstriped(offs):
    return offs[:16].T.reshape(-1).astype(np.int64)


def gelu(v):
    return 0.5 * v * (1.0 + np.tanh(np.sqrt(2.0 / np.pi) * (v + 0.044715 * v**3)))


K, T, S, V, N = 512, 2048, 512, 512, 1024


def setup_inputs():
    n = np.random.standard_normal
    s = mx_kscale(K)[:, None]
    return {
        "xT": (n((K, T)) * s).astype(np.float32),
        "w": (n((K, N)) / np.sqrt(K) / s).astype(np.float32),
        "b": (0.3 * n((V, 1))).astype(np.float32),
        "offs": striped(np.random.permutation(T)[:S]),
        "pos1": striped(np.random.permutation(N)[:V]),
    }


def reference(xT, w, b, offs, pos1):
    y = mxq(f64(w)[:, unstriped(pos1)], 0, "e4m3").T @ mxq(f64(xT)[:, unstriped(offs)], 0, "e4m3")
    return gelu(y + f64(b))

@@ -1,0 +1,122 @@
+from contextlib import ExitStack
+
+import concourse.mybir as mybir
+from concourse.masks import make_identity
+
+K, T, S, V, N = 512, 2048, 512, 512, 1024
+FLOPS = 2 * K * S * V
+
+F32 = mybir.dt.float32
+BF16 = mybir.dt.bfloat16
+U32 = mybir.dt.uint32
+U16 = mybir.dt.uint16
+U8 = mybir.dt.uint8
+FP8X4 = mybir.dt.float8_e4m3fn_x4
+GELU = mybir.ActivationFunctionType.Gelu_apprx_tanh
+
+P = 128
+PACK = 4
+LIST_ROWS = 16
+W_TILES = V // P
+TOKENS = 256
+X_SLICES = S // TOKENS
+
+
+def tile_picked_cross_gelu_l_kernel(tc, xT, w, b, offs, pos1, out):
+    nc = tc.nc
+    x_planes = xT.rearrange("(p t) c -> p t c", t=PACK)
+    w_planes = w.rearrange("(p t) c -> p t c", t=PACK)
+
+    with ExitStack() as ctx:
+        keep = ctx.enter_context(tc.tile_pool(name="keep", bufs=1))
+        psum = ctx.enter_context(tc.psum_pool(name="psum", bufs=1))
+
+        warm = keep.tile([P, 8], F32, name="warm")
+        nc.vector.memset(warm[:], 0.0)
+        warm_out = keep.tile([P, 8], F32, name="warm_out")
+        nc.scalar.activation(warm_out[:], warm[:], GELU)
+
+        pos1_sb = keep.tile([P, V // LIST_ROWS], U16, name="pos1_sb")
+        offs_sb = keep.tile([P, S // LIST_ROWS], U16, name="offs_sb")
+        w_sb = [keep.tile([P, 2, N], F32, name=f"w{u}") for u in range(2)]
+        x_sb = [keep.tile([P, T], F32, name=f"x{t}") for t in range(PACK)]
+        b_rows = keep.tile([P, P], F32, name="b_rows")
+        nc.vector.memset(b_rows[:], 0.0)
+        ident = keep.tile([P, P], F32, name="ident")
+        make_identity(nc, ident[:])
+        nc.sync.dma_start(w_sb[0][:], w_planes[:, 0:2, :])
+        nc.sync.dma_start(pos1_sb[:], pos1)
+        nc.sync.dma_start(w_sb[1][:], w_planes[:, 2:4, :])
+        nc.sync.dma_start(offs_sb[:], offs)
+        nc.sync.dma_start(b_rows[0:W_TILES, :], b.rearrange("(m p) o -> m (p o)", p=P))
+        for t in range(PACK):
+            nc.sync.dma_start(x_sb[t][:], x_planes[:, t, :])
+
+        b_turned = psum.tile([P, TOKENS], F32, name="acc7")
+        nc.tensor.transpose(b_turned[:, 0:P], b_rows[:], ident[:])
+        b_sb = keep.tile([P, W_TILES], F32, name="b_sb")
+        nc.vector.tensor_copy(b_sb[:], b_turned[:, 0:W_TILES])
+
+        w_grouped = keep.tile([P, V, PACK], BF16, name="w_grouped", align_bytes=64)
+        w_words = w_grouped[:].rearrange("p n t -> p (n t)").bitcast(U32).rearrange("p (n u) -> p n u", u=2)
+        w_codes = keep.tile([P, V], U32, name="w_codes", align_bytes=64)
+        w_scales = keep.tile([P, V], U8, name="w_scales", align_bytes=64)
+        for u in range(2):
+            w_pair = keep.tile([P, N, 2], BF16, name=f"w_pair{u}", align_bytes=64)
+            nc.scalar.copy(w_pair[:], w_sb[u][:].rearrange("p e c -> p c e"))
+            nc.vector.tensor_copy(
+                w_words[:, :, u],
+                w_pair[:].rearrange("p c e -> p (c e)").bitcast(U32).indirect(pos1_sb[:]),
+            )
+        for m in range(W_TILES):
+            cols = slice(m * P, (m + 1) * P)
+            nc.vector.quantize_mx(
+                out=w_codes[:, cols].bitcast(FP8X4),
+                scales=w_scales[:, cols],
+                in_=w_grouped[:, cols, :].rearrange("p n t -> p (n t)"),
+            )
+
+        x_grouped = keep.tile([P, S, PACK], BF16, name="x_grouped", align_bytes=64)
+        x_codes = keep.tile([P, S], U32, name="x_codes", align_bytes=64)
+        x_scales = keep.tile([P, S], U8, name="x_scales", align_bytes=64)
+
+        banks = [1, 0, 7, 6, 5, 4, 3, 2, 1, 0]
+        x_got = keep.tile([P, 2, S], F32, name="x_got")
+        for t in range(2):
+            nc.vector.tensor_copy(x_got[:, t, :], x_sb[t][:].indirect(offs_sb[:]))
+        nc.scalar.copy(x_grouped[:, :, 0:2], x_got[:].rearrange("p t n -> p n t"))
+        nc.vector.tensor_copy(x_grouped[:, :, 2], x_sb[2][:].indirect(offs_sb[:]))
+        for s in range(X_SLICES):
+            toks = slice(s * TOKENS, (s + 1) * TOKENS)
+            entries = slice(s * TOKENS // LIST_ROWS, (s + 1) * TOKENS // LIST_ROWS)
+            nc.vector.tensor_copy(x_grouped[:, toks, PACK - 1], x_sb[PACK - 1][:].indirect(offs_sb[:, entries]))
+            if s + 1 < X_SLICES:
+                nc.gpsimd.tensor_copy(
+                    x_grouped[:, (s + 1) * TOKENS : (s + 1) * TOKENS + 2, PACK - 1],
+                    x_grouped[:, s * TOKENS : s * TOKENS + 2, PACK - 1],
+                )
+            for c0 in (toks.start, toks.start + P):
+                part = slice(c0, c0 + P)
+                nc.vector.quantize_mx(
+                    out=x_codes[:, part].bitcast(FP8X4),
+                    scales=x_scales[:, part],
+                    in_=x_grouped[:, part, :].rearrange("p n t -> p (n t)"),
+                )
+            for m in range(W_TILES):
+                words = slice(m * P, (m + 1) * P)
+                res = keep.tile([P, TOKENS], F32, name=f"res{s}_{m}")
+                for c0 in range(0, TOKENS, P if m == 0 else TOKENS):
+                    width = P if m == 0 else TOKENS
+                    part = slice(toks.start + c0, toks.start + c0 + width)
+                    acc = psum.tile([P, TOKENS], F32, name=f"acc{banks.pop()}")
+                    nc.tensor.matmul_mx(
+                        out=acc[:, 0:width],
+                        lhsT=w_codes[:, words].bitcast(FP8X4),
+                        lhsT_scale=w_scales[:, words],
+                        rhs=x_codes[:, part].bitcast(FP8X4),
+                        rhs_scale=x_scales[:, part],
+                        start=True,
+                        stop=True,
+                    )
+                    nc.scalar.activation(res[:, c0 : c0 + width], acc[:, 0:width], GELU, bias=b_sb[:, m : m + 1])
+                nc.sync.dma_start(out[words, toks], res[:])

@@ -13,19 +13,19 @@ U16 = mybir.dt.uint16
 U8 = mybir.dt.uint8
 FP8X4 = mybir.dt.float8_e4m3fn_x4
 GELU = mybir.ActivationFunctionType.Gelu_apprx_tanh
+COPY = mybir.ActivationFunctionType.Copy
 
 P = 128
 PACK = 4
 LIST_ROWS = 16
 W_TILES = V // P
-TOKENS = 256
-X_SLICES = S // TOKENS
+HALF = S // 2
 
 
 def tile_picked_cross_gelu_l_kernel(tc, xT, w, b, offs, pos1, out):
     nc = tc.nc
-    x_planes = xT.rearrange("(p t) c -> p t c", t=PACK)
-    w_planes = w.rearrange("(p t) c -> p t c", t=PACK)
+    x_rows = xT.rearrange("(p t) c -> p t c", t=PACK)
+    w_rows = w.rearrange("(p t) c -> p t c", t=PACK)
 
     with ExitStack() as ctx:
         keep = ctx.enter_context(tc.tile_pool(name="keep", bufs=1))
@@ -38,85 +38,104 @@ def tile_picked_cross_gelu_l_kernel(tc, xT, w, b, offs, pos1, out):
 
         pos1_sb = keep.tile([P, V // LIST_ROWS], U16, name="pos1_sb")
         offs_sb = keep.tile([P, S // LIST_ROWS], U16, name="offs_sb")
-        w_sb = [keep.tile([P, 2, N], F32, name=f"w{u}") for u in range(2)]
+        w01 = keep.tile([P, 2, N], F32, name="w01")
+        w2 = [keep.tile([P, N // 2], F32, name=f"w2_{h}") for h in range(2)]
+        w3 = keep.tile([P, N], F32, name="w3")
         x_sb = [keep.tile([P, T], F32, name=f"x{t}") for t in range(PACK)]
         b_rows = keep.tile([P, P], F32, name="b_rows")
         nc.vector.memset(b_rows[:], 0.0)
         ident = keep.tile([P, P], F32, name="ident")
         make_identity(nc, ident[:])
-        nc.sync.dma_start(w_sb[0][:], w_planes[:, 0:2, :])
+        nc.sync.dma_start(w01[:], w_rows[:, 0:2, :])
         nc.sync.dma_start(pos1_sb[:], pos1)
-        nc.sync.dma_start(w_sb[1][:], w_planes[:, 2:4, :])
+        nc.sync.dma_start(x_sb[1][:], x_rows[:, 1, :])
         nc.sync.dma_start(offs_sb[:], offs)
         nc.sync.dma_start(b_rows[0:W_TILES, :], b.rearrange("(m p) o -> m (p o)", p=P))
-        for t in range(PACK):
-            nc.sync.dma_start(x_sb[t][:], x_planes[:, t, :])
+        for t in (2, 0, 3):
+            nc.sync.dma_start(x_sb[t][:], x_rows[:, t, :])
+        for h in range(2):
+            nc.sync.dma_start(w2[h][:], w_rows[:, 2, h * N // 2 : (h + 1) * N // 2])
+        nc.sync.dma_start(w3[:], w_rows[:, 3, :])
 
-        b_turned = psum.tile([P, TOKENS], F32, name="acc7")
+        b_turned = psum.tile([P, HALF], F32, name="acc7")
         nc.tensor.transpose(b_turned[:, 0:P], b_rows[:], ident[:])
         b_sb = keep.tile([P, W_TILES], F32, name="b_sb")
         nc.vector.tensor_copy(b_sb[:], b_turned[:, 0:W_TILES])
 
         w_grouped = keep.tile([P, V, PACK], BF16, name="w_grouped", align_bytes=64)
-        w_words = w_grouped[:].rearrange("p n t -> p (n t)").bitcast(U32).rearrange("p (n u) -> p n u", u=2)
         w_codes = keep.tile([P, V], U32, name="w_codes", align_bytes=64)
         w_scales = keep.tile([P, V], U8, name="w_scales", align_bytes=64)
-        for u in range(2):
-            w_pair = keep.tile([P, N, 2], BF16, name=f"w_pair{u}", align_bytes=64)
-            nc.scalar.copy(w_pair[:], w_sb[u][:].rearrange("p e c -> p c e"))
-            nc.vector.tensor_copy(
-                w_words[:, :, u],
-                w_pair[:].rearrange("p c e -> p (c e)").bitcast(U32).indirect(pos1_sb[:]),
-            )
-        for m in range(W_TILES):
-            cols = slice(m * P, (m + 1) * P)
-            nc.vector.quantize_mx(
-                out=w_codes[:, cols].bitcast(FP8X4),
-                scales=w_scales[:, cols],
-                in_=w_grouped[:, cols, :].rearrange("p n t -> p (n t)"),
-            )
+        w1_bf = keep.tile([P, N], BF16, name="w1_bf", align_bytes=64)
+        w2_bf = keep.tile([P, N], BF16, name="w2_bf", align_bytes=64)
+        nc.scalar.copy(w1_bf[:], w01[:, 1, :])
+        nc.scalar.activation(w_grouped[:, :, 0], w1_bf[:].indirect(pos1_sb[:]), COPY)
+        nc.vector.tensor_copy(w_grouped[:, :, 2], w01[:, 0, :].indirect(pos1_sb[:]))
 
         x_grouped = keep.tile([P, S, PACK], BF16, name="x_grouped", align_bytes=64)
         x_codes = keep.tile([P, S], U32, name="x_codes", align_bytes=64)
         x_scales = keep.tile([P, S], U8, name="x_scales", align_bytes=64)
-
-        banks = [1, 0, 7, 6, 5, 4, 3, 2, 1, 0]
         x_got = keep.tile([P, 2, S], F32, name="x_got")
         for t in range(2):
-            nc.vector.tensor_copy(x_got[:, t, :], x_sb[t][:].indirect(offs_sb[:]))
+            nc.vector.tensor_copy(x_got[:, t, :], x_sb[1 + t][:].indirect(offs_sb[:]))
         nc.scalar.copy(x_grouped[:, :, 0:2], x_got[:].rearrange("p t n -> p n t"))
-        nc.vector.tensor_copy(x_grouped[:, :, 2], x_sb[2][:].indirect(offs_sb[:]))
-        for s in range(X_SLICES):
-            toks = slice(s * TOKENS, (s + 1) * TOKENS)
-            entries = slice(s * TOKENS // LIST_ROWS, (s + 1) * TOKENS // LIST_ROWS)
-            nc.vector.tensor_copy(x_grouped[:, toks, PACK - 1], x_sb[PACK - 1][:].indirect(offs_sb[:, entries]))
-            if s + 1 < X_SLICES:
+        nc.vector.tensor_copy(x_grouped[:, :, 2], x_sb[0][:].indirect(offs_sb[:]))
+        for s in range(2):
+            toks = slice(s * HALF, (s + 1) * HALF)
+            entries = slice(s * HALF // LIST_ROWS, (s + 1) * HALF // LIST_ROWS)
+            nc.vector.tensor_copy(x_grouped[:, toks, 3], x_sb[3][:].indirect(offs_sb[:, entries]))
+        for s in range(2):
+            toks = slice(s * HALF, (s + 1) * HALF)
+            nc.vector.quantize_mx(
+                out=x_codes[:, toks].bitcast(FP8X4),
+                scales=x_scales[:, toks],
+                in_=x_grouped[:, toks, :].rearrange("p n t -> p (n t)"),
+            )
+
+        for h in range(2):
+            nc.scalar.copy(w2_bf[:, h * N // 2 : (h + 1) * N // 2], w2[h][:])
+        for m in range(W_TILES):
+            words = slice(m * P, (m + 1) * P)
+            entries = slice(m * P // LIST_ROWS, (m + 1) * P // LIST_ROWS)
+            nc.scalar.activation(w_grouped[:, words, 1], w2_bf[:].indirect(pos1_sb[:, entries]), COPY)
+
+        def look_up(m):
+            words = slice(m * P, (m + 1) * P)
+            entries = slice(m * P // LIST_ROWS, (m + 1) * P // LIST_ROWS)
+            nc.vector.tensor_copy(w_grouped[:, words, 3], w3[:].indirect(pos1_sb[:, entries]))
+
+        banks = [1, 0, 7, 6, 5, 4, 3, 2, 1, 0]
+        look_up(0)
+        look_up(1)
+        for m in range(W_TILES):
+            words = slice(m * P, (m + 1) * P)
+            if m + 2 < W_TILES:
                 nc.gpsimd.tensor_copy(
-                    x_grouped[:, (s + 1) * TOKENS : (s + 1) * TOKENS + 2, PACK - 1],
-                    x_grouped[:, s * TOKENS : s * TOKENS + 2, PACK - 1],
+                    w_grouped[:, (m + 2) * P : (m + 2) * P + 2, 3],
+                    w_grouped[:, m * P, 1:4:2],
                 )
-            for c0 in (toks.start, toks.start + P):
-                part = slice(c0, c0 + P)
-                nc.vector.quantize_mx(
-                    out=x_codes[:, part].bitcast(FP8X4),
-                    scales=x_scales[:, part],
-                    in_=x_grouped[:, part, :].rearrange("p n t -> p (n t)"),
+            nc.vector.quantize_mx(
+                out=w_codes[:, words].bitcast(FP8X4),
+                scales=w_scales[:, words],
+                in_=w_grouped[:, words, :].rearrange("p n t -> p (n t)"),
+            )
+            if m + 2 < W_TILES:
+                look_up(m + 2)
+            res = keep.tile([P, S], F32, name=f"res{m}")
+            cuts = [0, P, HALF, S] if m == 0 else [0, HALF, HALF + P, S] if m == W_TILES - 1 else [0, HALF, S]
+            stores = [HALF, S] if m in (0, W_TILES - 1) else [S]
+            stored = 0
+            for c0, c1 in zip(cuts, cuts[1:]):
+                acc = psum.tile([P, HALF], F32, name=f"acc{banks.pop()}")
+                nc.tensor.matmul_mx(
+                    out=acc[:, 0 : c1 - c0],
+                    lhsT=w_codes[:, words].bitcast(FP8X4),
+                    lhsT_scale=w_scales[:, words],
+                    rhs=x_codes[:, c0:c1].bitcast(FP8X4),
+                    rhs_scale=x_scales[:, c0:c1],
+                    start=True,
+                    stop=True,
                 )
-            for m in range(W_TILES):
-                words = slice(m * P, (m + 1) * P)
-                res = keep.tile([P, TOKENS], F32, name=f"res{s}_{m}")
-                for c0 in range(0, TOKENS, P if m == 0 else TOKENS):
-                    width = P if m == 0 else TOKENS
-                    part = slice(toks.start + c0, toks.start + c0 + width)
-                    acc = psum.tile([P, TOKENS], F32, name=f"acc{banks.pop()}")
-                    nc.tensor.matmul_mx(
-                        out=acc[:, 0:width],
-                        lhsT=w_codes[:, words].bitcast(FP8X4),
-                        lhsT_scale=w_scales[:, words],
-                        rhs=x_codes[:, part].bitcast(FP8X4),
-                        rhs_scale=x_scales[:, part],
-                        start=True,
-                        stop=True,
-                    )
-                    nc.scalar.activation(res[:, c0 : c0 + width], acc[:, 0:width], GELU, bias=b_sb[:, m : m + 1])
-                nc.sync.dma_start(out[words, toks], res[:])
+                nc.scalar.activation(res[:, c0:c1], acc[:, 0 : c1 - c0], GELU, bias=b_sb[:, m : m + 1])
+                if c1 in stores:
+                    nc.sync.dma_start(out[words, stored:c1], res[:, stored:c1])
+                    stored = c1

@@ -93,36 +93,33 @@ def tile_picked_cross_gelu_l_kernel(tc, xT, w, b, offs, pos1, out):
 
         for h in range(2):
             nc.scalar.copy(w2_bf[:, h * N // 2 : (h + 1) * N // 2], w2[h][:])
-        for m in range(W_TILES):
+        order = [0, 3, 1, 2]
+        for m in order:
             words = slice(m * P, (m + 1) * P)
             entries = slice(m * P // LIST_ROWS, (m + 1) * P // LIST_ROWS)
             nc.scalar.activation(w_grouped[:, words, 1], w2_bf[:].indirect(pos1_sb[:, entries]), COPY)
 
         def look_up(m):
-            words = slice(m * P, (m + 1) * P)
-            entries = slice(m * P // LIST_ROWS, (m + 1) * P // LIST_ROWS)
+            end = (m + 1) * P + (LIST_ROWS if m < 2 else 0)
+            words = slice(m * P, end)
+            entries = slice(m * P // LIST_ROWS, end // LIST_ROWS)
             nc.vector.tensor_copy(w_grouped[:, words, 3], w3[:].indirect(pos1_sb[:, entries]))
 
         banks = [1, 0, 7, 6, 5, 4, 3, 2, 1, 0]
-        look_up(0)
-        look_up(1)
-        for m in range(W_TILES):
+        look_up(order[0])
+        look_up(order[1])
+        for i, m in enumerate(order):
             words = slice(m * P, (m + 1) * P)
-            if m + 2 < W_TILES:
-                nc.gpsimd.tensor_copy(
-                    w_grouped[:, (m + 2) * P : (m + 2) * P + 2, 3],
-                    w_grouped[:, m * P, 1:4:2],
-                )
             nc.vector.quantize_mx(
                 out=w_codes[:, words].bitcast(FP8X4),
                 scales=w_scales[:, words],
                 in_=w_grouped[:, words, :].rearrange("p n t -> p (n t)"),
             )
-            if m + 2 < W_TILES:
-                look_up(m + 2)
+            if i + 2 < W_TILES:
+                look_up(order[i + 2])
             res = keep.tile([P, S], F32, name=f"res{m}")
-            cuts = [0, P, HALF, S] if m == 0 else [0, HALF, HALF + P, S] if m == W_TILES - 1 else [0, HALF, S]
-            stores = [HALF, S] if m in (0, W_TILES - 1) else [S]
+            cuts = [0, P, HALF, S] if i == 0 else [0, HALF, HALF + P, S] if i == W_TILES - 1 else [0, HALF, S]
+            stores = [HALF, S] if i in (0, W_TILES - 1) else [S]
             stored = 0
             for c0, c1 in zip(cuts, cuts[1:]):
                 acc = psum.tile([P, HALF], F32, name=f"acc{banks.pop()}")

@@ -1,7 +1,6 @@
 from contextlib import ExitStack
 
 import concourse.mybir as mybir
-from concourse.masks import make_identity
 
 K, T, S, V, N = 512, 2048, 512, 512, 1024
 FLOPS = 2 * K * S * V
@@ -41,26 +40,21 @@ def tile_picked_cross_gelu_l_kernel(tc, xT, w, b, offs, pos1, out):
         w01 = keep.tile([P, 2, N], F32, name="w01")
         w2 = [keep.tile([P, N // 2], F32, name=f"w2_{h}") for h in range(2)]
         w3 = keep.tile([P, N], F32, name="w3")
-        x_sb = [keep.tile([P, T], F32, name=f"x{t}") for t in range(PACK)]
-        b_rows = keep.tile([P, P], F32, name="b_rows")
-        nc.vector.memset(b_rows[:], 0.0)
-        ident = keep.tile([P, P], F32, name="ident")
-        make_identity(nc, ident[:])
+        x12 = keep.tile([P, 2, T], F32, name="x12")
+        x0 = keep.tile([P, T], F32, name="x0")
+        x3 = keep.tile([P, T], F32, name="x3")
+        b_sb = keep.tile([P, W_TILES], F32, name="b_sb")
         nc.sync.dma_start(w01[:], w_rows[:, 0:2, :])
         nc.sync.dma_start(pos1_sb[:], pos1)
-        nc.sync.dma_start(x_sb[1][:], x_rows[:, 1, :])
+        nc.sync.dma_start(x12[:], x_rows[:, 1:3, :])
         nc.sync.dma_start(offs_sb[:], offs)
-        nc.sync.dma_start(b_rows[0:W_TILES, :], b.rearrange("(m p) o -> m (p o)", p=P))
-        for t in (2, 0, 3):
-            nc.sync.dma_start(x_sb[t][:], x_rows[:, t, :])
+        nc.sync.dma_start(x0[:], x_rows[:, 0, :])
+        nc.sync.dma_start(x3[:], x_rows[:, 3, :])
         for h in range(2):
             nc.sync.dma_start(w2[h][:], w_rows[:, 2, h * N // 2 : (h + 1) * N // 2])
         nc.sync.dma_start(w3[:], w_rows[:, 3, :])
-
-        b_turned = psum.tile([P, HALF], F32, name="acc7")
-        nc.tensor.transpose(b_turned[:, 0:P], b_rows[:], ident[:])
-        b_sb = keep.tile([P, W_TILES], F32, name="b_sb")
-        nc.vector.tensor_copy(b_sb[:], b_turned[:, 0:W_TILES])
+        with nc.allow_non_contiguous_dma(reason="one bias value a partition and word tile"):
+            nc.sync.dma_start(b_sb[:], b.rearrange("(m p) o -> p (m o)", p=P))
 
         w_grouped = keep.tile([P, V, PACK], BF16, name="w_grouped", align_bytes=64)
         w_codes = keep.tile([P, V], U32, name="w_codes", align_bytes=64)
@@ -76,13 +70,13 @@ def tile_picked_cross_gelu_l_kernel(tc, xT, w, b, offs, pos1, out):
         x_scales = keep.tile([P, S], U8, name="x_scales", align_bytes=64)
         x_got = keep.tile([P, 2, S], F32, name="x_got")
         for t in range(2):
-            nc.vector.tensor_copy(x_got[:, t, :], x_sb[1 + t][:].indirect(offs_sb[:]))
+            nc.vector.tensor_copy(x_got[:, t, :], x12[:, t, :].indirect(offs_sb[:]))
         nc.scalar.copy(x_grouped[:, :, 0:2], x_got[:].rearrange("p t n -> p n t"))
-        nc.vector.tensor_copy(x_grouped[:, :, 2], x_sb[0][:].indirect(offs_sb[:]))
+        nc.vector.tensor_copy(x_grouped[:, :, 2], x0[:].indirect(offs_sb[:]))
         for s in range(2):
             toks = slice(s * HALF, (s + 1) * HALF)
             entries = slice(s * HALF // LIST_ROWS, (s + 1) * HALF // LIST_ROWS)
-            nc.vector.tensor_copy(x_grouped[:, toks, 3], x_sb[3][:].indirect(offs_sb[:, entries]))
+            nc.vector.tensor_copy(x_grouped[:, toks, 3], x3[:].indirect(offs_sb[:, entries]))
         for s in range(2):
             toks = slice(s * HALF, (s + 1) * HALF)
             nc.vector.quantize_mx(
@@ -105,7 +99,7 @@ def tile_picked_cross_gelu_l_kernel(tc, xT, w, b, offs, pos1, out):
             entries = slice(m * P // LIST_ROWS, end // LIST_ROWS)
             nc.vector.tensor_copy(w_grouped[:, words, 3], w3[:].indirect(pos1_sb[:, entries]))
 
-        banks = [1, 0, 7, 6, 5, 4, 3, 2, 1, 0]
+        banks = [3, 2, 1, 0, 7, 6, 5, 4, 3, 2, 1, 0]
         look_up(order[0])
         look_up(order[1])
         for i, m in enumerate(order):

@@ -30,11 +30,6 @@ def tile_picked_cross_gelu_l_kernel(tc, xT, w, b, offs, pos1, out):
         keep = ctx.enter_context(tc.tile_pool(name="keep", bufs=1))
         psum = ctx.enter_context(tc.psum_pool(name="psum", bufs=1))
 
-        warm = keep.tile([P, 8], F32, name="warm")
-        nc.vector.memset(warm[:], 0.0)
-        warm_out = keep.tile([P, 8], F32, name="warm_out")
-        nc.scalar.activation(warm_out[:], warm[:], GELU)
-
         pos1_sb = keep.tile([P, V // LIST_ROWS], U16, name="pos1_sb")
         offs_sb = keep.tile([P, S // LIST_ROWS], U16, name="offs_sb")
         w01 = keep.tile([P, 2, N], F32, name="w01")
@@ -44,10 +39,10 @@ def tile_picked_cross_gelu_l_kernel(tc, xT, w, b, offs, pos1, out):
         x0 = keep.tile([P, T], F32, name="x0")
         x3 = keep.tile([P, T], F32, name="x3")
         b_sb = keep.tile([P, W_TILES], F32, name="b_sb")
-        nc.sync.dma_start(w01[:], w_rows[:, 0:2, :])
+        nc.scalar.dma_start(w01[:], w_rows[:, 0:2, :])
         nc.sync.dma_start(pos1_sb[:], pos1)
-        nc.sync.dma_start(x12[:], x_rows[:, 1:3, :])
         nc.sync.dma_start(offs_sb[:], offs)
+        nc.sync.dma_start(x12[:], x_rows[:, 1:3, :])
         nc.sync.dma_start(x0[:], x_rows[:, 0, :])
         nc.sync.dma_start(x3[:], x_rows[:, 3, :])
         for h in range(2):
@@ -55,6 +50,11 @@ def tile_picked_cross_gelu_l_kernel(tc, xT, w, b, offs, pos1, out):
         nc.sync.dma_start(w3[:], w_rows[:, 3, :])
         with nc.allow_non_contiguous_dma(reason="one bias value a partition and word tile"):
             nc.sync.dma_start(b_sb[:], b.rearrange("(m p) o -> p (m o)", p=P))
+
+        warm = keep.tile([P, 8], F32, name="warm")
+        nc.vector.memset(warm[:], 0.0)
+        warm_out = keep.tile([P, 8], F32, name="warm_out")
+        nc.scalar.activation(warm_out[:], warm[:], GELU)
 
         w_grouped = keep.tile([P, V, PACK], BF16, name="w_grouped", align_bytes=64)
         w_codes = keep.tile([P, V], U32, name="w_codes", align_bytes=64)

@@ -19,6 +19,7 @@ PACK = 4
 LIST_ROWS = 16
 W_TILES = V // P
 HALF = S // 2
+BLOCK = 32
 
 
 def tile_picked_cross_gelu_l_kernel(tc, xT, w, b, offs, pos1, out):
@@ -38,8 +39,14 @@ def tile_picked_cross_gelu_l_kernel(tc, xT, w, b, offs, pos1, out):
         x12 = keep.tile([P, 2, T], F32, name="x12")
         x0 = keep.tile([P, T], F32, name="x0")
         x3 = keep.tile([P, T], F32, name="x3")
-        b_sb = keep.tile([P, W_TILES], F32, name="b_sb")
+        b_rows = keep.tile([P, P], F32, name="b_rows", align_bytes=64)
+        b_cols = keep.tile([P, P], F32, name="b_cols", align_bytes=64)
+        nc.vector.memset(b_rows[:], 0.0)
         nc.scalar.dma_start(w01[:], w_rows[:, 0:2, :])
+        nc.scalar.dma_start(
+            b_rows[0:P:BLOCK, :].rearrange("q (m j) -> q m j", j=BLOCK),
+            b.rearrange("(m q j) o -> q m (j o)", m=W_TILES, j=BLOCK),
+        )
         nc.sync.dma_start(pos1_sb[:], pos1)
         nc.sync.dma_start(offs_sb[:], offs)
         nc.sync.dma_start(x12[:], x_rows[:, 1:3, :])
@@ -48,8 +55,7 @@ def tile_picked_cross_gelu_l_kernel(tc, xT, w, b, offs, pos1, out):
         for h in range(2):
             nc.sync.dma_start(w2[h][:], w_rows[:, 2, h * N // 2 : (h + 1) * N // 2])
         nc.sync.dma_start(w3[:], w_rows[:, 3, :])
-        with nc.allow_non_contiguous_dma(reason="one bias value a partition and word tile"):
-            nc.sync.dma_start(b_sb[:], b.rearrange("(m p) o -> p (m o)", p=P))
+        nc.vector.transpose(b_cols[:], b_rows[:])
 
         warm = keep.tile([P, 8], F32, name="warm")
         nc.vector.memset(warm[:], 0.0)
@@ -126,7 +132,7 @@ def tile_picked_cross_gelu_l_kernel(tc, xT, w, b, offs, pos1, out):
                     start=True,
                     stop=True,
                 )
-                nc.scalar.activation(res[:, c0:c1], acc[:, 0 : c1 - c0], GELU, bias=b_sb[:, m : m + 1])
+                nc.scalar.activation(res[:, c0:c1], acc[:, 0 : c1 - c0], GELU, bias=b_cols[:, m * BLOCK : m * BLOCK + 1])
                 if c1 in stores:
                     nc.sync.dma_start(out[words, stored:c1], res[:, stored:c1])
                     stored = c1

@@ -41,7 +41,7 @@ def tile_picked_cross_gelu_l_kernel(tc, xT, w, b, offs, pos1, out):
         x3 = keep.tile([P, T], F32, name="x3")
         b_rows = keep.tile([P, P], F32, name="b_rows", align_bytes=64)
         b_cols = keep.tile([P, P], F32, name="b_cols", align_bytes=64)
-        nc.vector.memset(b_rows[:], 0.0)
+        nc.gpsimd.memset(b_rows[:], 0.0)
         nc.scalar.dma_start(w01[:], w_rows[:, 0:2, :])
         nc.scalar.dma_start(
             b_rows[0:P:BLOCK, :].rearrange("q (m j) -> q m j", j=BLOCK),
@@ -93,7 +93,7 @@ def tile_picked_cross_gelu_l_kernel(tc, xT, w, b, offs, pos1, out):
 
         for h in range(2):
             nc.scalar.copy(w2_bf[:, h * N // 2 : (h + 1) * N // 2], w2[h][:])
-        order = [0, 3, 1, 2]
+        order = [1, 3, 2, 0]
         for m in order:
             words = slice(m * P, (m + 1) * P)
             entries = slice(m * P // LIST_ROWS, (m + 1) * P // LIST_ROWS)

@@ -34,7 +34,7 @@ def tile_picked_cross_gelu_l_kernel(tc, xT, w, b, offs, pos1, out):
         pos1_sb = keep.tile([P, V // LIST_ROWS], U16, name="pos1_sb")
         offs_sb = keep.tile([P, S // LIST_ROWS], U16, name="offs_sb")
         w01 = keep.tile([P, 2, N], F32, name="w01")
-        w2 = [keep.tile([P, N // 2], F32, name=f"w2_{h}") for h in range(2)]
+        w2 = keep.tile([P, N], F32, name="w2")
         w3 = keep.tile([P, N], F32, name="w3")
         x12 = keep.tile([P, 2, T], F32, name="x12")
         x0 = keep.tile([P, T], F32, name="x0")
@@ -52,8 +52,7 @@ def tile_picked_cross_gelu_l_kernel(tc, xT, w, b, offs, pos1, out):
         nc.sync.dma_start(x12[:], x_rows[:, 1:3, :])
         nc.sync.dma_start(x0[:], x_rows[:, 0, :])
         nc.sync.dma_start(x3[:], x_rows[:, 3, :])
-        for h in range(2):
-            nc.sync.dma_start(w2[h][:], w_rows[:, 2, h * N // 2 : (h + 1) * N // 2])
+        nc.sync.dma_start(w2[:], w_rows[:, 2, :])
         nc.sync.dma_start(w3[:], w_rows[:, 3, :])
         nc.vector.transpose(b_cols[:], b_rows[:])
 
@@ -91,8 +90,9 @@ def tile_picked_cross_gelu_l_kernel(tc, xT, w, b, offs, pos1, out):
                 in_=x_grouped[:, toks, :].rearrange("p n t -> p (n t)"),
             )
 
-        for h in range(2):
-            nc.scalar.copy(w2_bf[:, h * N // 2 : (h + 1) * N // 2], w2[h][:])
+        share = 3 * N // 4
+        nc.scalar.copy(w2_bf[:, 0:share], w2[:, 0:share])
+        nc.gpsimd.tensor_copy(w2_bf[:, share:N], w2[:, share:N])
         order = [1, 3, 2, 0]
         for m in order:
             words = slice(m * P, (m + 1) * P)
@@ -119,7 +119,7 @@ def tile_picked_cross_gelu_l_kernel(tc, xT, w, b, offs, pos1, out):
                 look_up(order[i + 2])
             res = keep.tile([P, S], F32, name=f"res{m}")
             cuts = [0, P, HALF, S] if i == 0 else [0, HALF, HALF + P, S] if i == W_TILES - 1 else [0, HALF, S]
-            stores = [HALF, S] if i in (0, W_TILES - 1) else [S]
+            stores = cuts[1:] if i == 0 else [HALF, S] if i == W_TILES - 1 else [S]
             stored = 0
             for c0, c1 in zip(cuts, cuts[1:]):
                 acc = psum.tile([P, HALF], F32, name=f"acc{banks.pop()}")

@@ -31,15 +31,15 @@ def tile_picked_cross_gelu_l_kernel(tc, xT, w, b, offs, pos1, out):
         keep = ctx.enter_context(tc.tile_pool(name="keep", bufs=1))
         psum = ctx.enter_context(tc.psum_pool(name="psum", bufs=1))
 
-        pos1_sb = keep.tile([P, V // LIST_ROWS], U16, name="pos1_sb")
-        offs_sb = keep.tile([P, S // LIST_ROWS], U16, name="offs_sb")
-        w01 = keep.tile([P, 2, N], F32, name="w01")
-        w2 = keep.tile([P, N], F32, name="w2")
-        w3 = keep.tile([P, N], F32, name="w3")
-        x12 = keep.tile([P, 2, T], F32, name="x12")
-        x0 = keep.tile([P, T], F32, name="x0")
-        x3 = keep.tile([P, T], F32, name="x3")
-        b_rows = keep.tile([P, P], F32, name="b_rows", align_bytes=64)
+        pos1_sb = keep.tile([P, V // LIST_ROWS], U16, name="pos1_sb", align_bytes=256)
+        offs_sb = keep.tile([P, S // LIST_ROWS], U16, name="offs_sb", align_bytes=256)
+        w01 = keep.tile([P, 2, N], F32, name="w01", align_bytes=256)
+        w2 = keep.tile([P, N], F32, name="w2", align_bytes=256)
+        w3 = keep.tile([P, N], F32, name="w3", align_bytes=256)
+        x12 = keep.tile([P, 2, T], F32, name="x12", align_bytes=256)
+        x0 = keep.tile([P, T], F32, name="x0", align_bytes=256)
+        x3 = keep.tile([P, T], F32, name="x3", align_bytes=256)
+        b_rows = keep.tile([P, P], F32, name="b_rows", align_bytes=256)
         b_cols = keep.tile([P, P], F32, name="b_cols", align_bytes=64)
         nc.gpsimd.memset(b_rows[:], 0.0)
         nc.scalar.dma_start(w01[:], w_rows[:, 0:2, :])
@@ -117,7 +117,7 @@ def tile_picked_cross_gelu_l_kernel(tc, xT, w, b, offs, pos1, out):
             )
             if i + 2 < W_TILES:
                 look_up(order[i + 2])
-            res = keep.tile([P, S], F32, name=f"res{m}")
+            res = keep.tile([P, S], F32, name=f"res{m}", align_bytes=256)
             cuts = [0, P, HALF, S] if i == 0 else [0, HALF, HALF + P, S] if i == W_TILES - 1 else [0, HALF, S]
             stores = cuts[1:] if i == 0 else [HALF, S] if i == W_TILES - 1 else [S]
             stored = 0

@@ -40,7 +40,7 @@ def tile_picked_cross_gelu_l_kernel(tc, xT, w, b, offs, pos1, out):
         x0 = keep.tile([P, T], F32, name="x0", align_bytes=256)
         x3 = keep.tile([P, T], F32, name="x3", align_bytes=256)
         b_rows = keep.tile([P, P], F32, name="b_rows", align_bytes=256)
-        b_cols = keep.tile([P, P], F32, name="b_cols", align_bytes=64)
+        b_cols = keep.tile([P, P], F32, name="b_cols", align_bytes=256)
         nc.gpsimd.memset(b_rows[:], 0.0)
         nc.scalar.dma_start(w01[:], w_rows[:, 0:2, :])
         nc.scalar.dma_start(
@@ -61,19 +61,19 @@ def tile_picked_cross_gelu_l_kernel(tc, xT, w, b, offs, pos1, out):
         warm_out = keep.tile([P, 8], F32, name="warm_out")
         nc.scalar.activation(warm_out[:], warm[:], GELU)
 
-        w_grouped = keep.tile([P, V, PACK], BF16, name="w_grouped", align_bytes=64)
-        w_codes = keep.tile([P, V], U32, name="w_codes", align_bytes=64)
-        w_scales = keep.tile([P, V], U8, name="w_scales", align_bytes=64)
-        w1_bf = keep.tile([P, N], BF16, name="w1_bf", align_bytes=64)
-        w2_bf = keep.tile([P, N], BF16, name="w2_bf", align_bytes=64)
+        w_grouped = keep.tile([P, V, PACK], BF16, name="w_grouped", align_bytes=256)
+        w_codes = keep.tile([P, V], U32, name="w_codes", align_bytes=256)
+        w_scales = keep.tile([P, V], U8, name="w_scales", align_bytes=256)
+        w1_bf = keep.tile([P, N], BF16, name="w1_bf", align_bytes=256)
+        w2_bf = keep.tile([P, N], BF16, name="w2_bf", align_bytes=256)
         nc.scalar.copy(w1_bf[:], w01[:, 1, :])
         nc.scalar.activation(w_grouped[:, :, 0], w1_bf[:].indirect(pos1_sb[:]), COPY)
         nc.vector.tensor_copy(w_grouped[:, :, 2], w01[:, 0, :].indirect(pos1_sb[:]))
 
-        x_grouped = keep.tile([P, S, PACK], BF16, name="x_grouped", align_bytes=64)
-        x_codes = keep.tile([P, S], U32, name="x_codes", align_bytes=64)
-        x_scales = keep.tile([P, S], U8, name="x_scales", align_bytes=64)
-        x_got = keep.tile([P, 2, S], F32, name="x_got")
+        x_grouped = keep.tile([P, S, PACK], BF16, name="x_grouped", align_bytes=256)
+        x_codes = keep.tile([P, S], U32, name="x_codes", align_bytes=256)
+        x_scales = keep.tile([P, S], U8, name="x_scales", align_bytes=256)
+        x_got = keep.tile([P, 2, S], F32, name="x_got", align_bytes=256)
         for t in range(2):
             nc.vector.tensor_copy(x_got[:, t, :], x12[:, t, :].indirect(offs_sb[:]))
         nc.scalar.copy(x_grouped[:, :, 0:2], x_got[:].rearrange("p t n -> p n t"))

@@ -118,8 +118,8 @@ def tile_picked_cross_gelu_l_kernel(tc, xT, w, b, offs, pos1, out):
             if i + 2 < W_TILES:
                 look_up(order[i + 2])
             res = keep.tile([P, S], F32, name=f"res{m}", align_bytes=256)
-            cuts = [0, P, HALF, S] if i == 0 else [0, HALF, HALF + P, S] if i == W_TILES - 1 else [0, HALF, S]
-            stores = cuts[1:] if i == 0 else [HALF, S] if i == W_TILES - 1 else [S]
+            cuts = [0, P, HALF, S] if i == 0 else [0, HALF, S]
+            stores = [S] if i == W_TILES - 1 else [HALF, S]
             stored = 0
             for c0, c1 in zip(cuts, cuts[1:]):
                 acc = psum.tile([P, HALF], F32, name=f"acc{banks.pop()}")

@@ -19,33 +19,39 @@ PACK = 4
 LIST_ROWS = 16
 W_TILES = V // P
 HALF = S // 2
-BLOCK = 32
+QUADRANT = 32
+BANKS = 8
+ALIGN = 256
+SCALAR_CAST = 3 * N // 4
 
 
 def tile_picked_cross_gelu_l_kernel(tc, xT, w, b, offs, pos1, out):
     nc = tc.nc
-    x_rows = xT.rearrange("(p t) c -> p t c", t=PACK)
-    w_rows = w.rearrange("(p t) c -> p t c", t=PACK)
+    x_rows = xT.rearrange("(p r) c -> p r c", r=PACK)
+    w_rows = w.rearrange("(p r) c -> p r c", r=PACK)
+
+    def entries(first, end):
+        return slice(first // LIST_ROWS, end // LIST_ROWS)
 
     with ExitStack() as ctx:
         keep = ctx.enter_context(tc.tile_pool(name="keep", bufs=1))
         psum = ctx.enter_context(tc.psum_pool(name="psum", bufs=1))
 
-        pos1_sb = keep.tile([P, V // LIST_ROWS], U16, name="pos1_sb", align_bytes=256)
-        offs_sb = keep.tile([P, S // LIST_ROWS], U16, name="offs_sb", align_bytes=256)
-        w01 = keep.tile([P, 2, N], F32, name="w01", align_bytes=256)
-        w2 = keep.tile([P, N], F32, name="w2", align_bytes=256)
-        w3 = keep.tile([P, N], F32, name="w3", align_bytes=256)
-        x12 = keep.tile([P, 2, T], F32, name="x12", align_bytes=256)
-        x0 = keep.tile([P, T], F32, name="x0", align_bytes=256)
-        x3 = keep.tile([P, T], F32, name="x3", align_bytes=256)
-        b_rows = keep.tile([P, P], F32, name="b_rows", align_bytes=256)
-        b_cols = keep.tile([P, P], F32, name="b_cols", align_bytes=256)
+        pos1_sb = keep.tile([P, V // LIST_ROWS], U16, name="pos1_sb", align_bytes=ALIGN)
+        offs_sb = keep.tile([P, S // LIST_ROWS], U16, name="offs_sb", align_bytes=ALIGN)
+        w01 = keep.tile([P, 2, N], F32, name="w01", align_bytes=ALIGN)
+        w2 = keep.tile([P, N], F32, name="w2", align_bytes=ALIGN)
+        w3 = keep.tile([P, N], F32, name="w3", align_bytes=ALIGN)
+        x12 = keep.tile([P, 2, T], F32, name="x12", align_bytes=ALIGN)
+        x0 = keep.tile([P, T], F32, name="x0", align_bytes=ALIGN)
+        x3 = keep.tile([P, T], F32, name="x3", align_bytes=ALIGN)
+        b_rows = keep.tile([P, P], F32, name="b_rows", align_bytes=ALIGN)
+        b_cols = keep.tile([P, P], F32, name="b_cols", align_bytes=ALIGN)
         nc.gpsimd.memset(b_rows[:], 0.0)
         nc.scalar.dma_start(w01[:], w_rows[:, 0:2, :])
         nc.scalar.dma_start(
-            b_rows[0:P:BLOCK, :].rearrange("q (m j) -> q m j", j=BLOCK),
-            b.rearrange("(m q j) o -> q m (j o)", m=W_TILES, j=BLOCK),
+            b_rows[0:P:QUADRANT, :].rearrange("q (m j) -> q m j", j=QUADRANT),
+            b.rearrange("(m q j) o -> q m (j o)", m=W_TILES, j=QUADRANT),
         )
         nc.sync.dma_start(pos1_sb[:], pos1)
         nc.sync.dma_start(offs_sb[:], offs)
@@ -61,53 +67,48 @@ def tile_picked_cross_gelu_l_kernel(tc, xT, w, b, offs, pos1, out):
         warm_out = keep.tile([P, 8], F32, name="warm_out")
         nc.scalar.activation(warm_out[:], warm[:], GELU)
 
-        w_grouped = keep.tile([P, V, PACK], BF16, name="w_grouped", align_bytes=256)
-        w_codes = keep.tile([P, V], U32, name="w_codes", align_bytes=256)
-        w_scales = keep.tile([P, V], U8, name="w_scales", align_bytes=256)
-        w1_bf = keep.tile([P, N], BF16, name="w1_bf", align_bytes=256)
-        w2_bf = keep.tile([P, N], BF16, name="w2_bf", align_bytes=256)
+        w_grouped = keep.tile([P, V, PACK], BF16, name="w_grouped", align_bytes=ALIGN)
+        w_codes = keep.tile([P, V], U32, name="w_codes", align_bytes=ALIGN)
+        w_scales = keep.tile([P, V], U8, name="w_scales", align_bytes=ALIGN)
+        w1_bf = keep.tile([P, N], BF16, name="w1_bf", align_bytes=ALIGN)
+        w2_bf = keep.tile([P, N], BF16, name="w2_bf", align_bytes=ALIGN)
         nc.scalar.copy(w1_bf[:], w01[:, 1, :])
         nc.scalar.activation(w_grouped[:, :, 0], w1_bf[:].indirect(pos1_sb[:]), COPY)
         nc.vector.tensor_copy(w_grouped[:, :, 2], w01[:, 0, :].indirect(pos1_sb[:]))
 
-        x_grouped = keep.tile([P, S, PACK], BF16, name="x_grouped", align_bytes=256)
-        x_codes = keep.tile([P, S], U32, name="x_codes", align_bytes=256)
-        x_scales = keep.tile([P, S], U8, name="x_scales", align_bytes=256)
-        x_got = keep.tile([P, 2, S], F32, name="x_got", align_bytes=256)
-        for t in range(2):
-            nc.vector.tensor_copy(x_got[:, t, :], x12[:, t, :].indirect(offs_sb[:]))
-        nc.scalar.copy(x_grouped[:, :, 0:2], x_got[:].rearrange("p t n -> p n t"))
+        x_grouped = keep.tile([P, S, PACK], BF16, name="x_grouped", align_bytes=ALIGN)
+        x_codes = keep.tile([P, S], U32, name="x_codes", align_bytes=ALIGN)
+        x_scales = keep.tile([P, S], U8, name="x_scales", align_bytes=ALIGN)
+        x12_picked = keep.tile([P, 2, S], F32, name="x12_picked", align_bytes=ALIGN)
+        for r in range(2):
+            nc.vector.tensor_copy(x12_picked[:, r, :], x12[:, r, :].indirect(offs_sb[:]))
+        nc.scalar.copy(x_grouped[:, :, 0:2], x12_picked[:].rearrange("p r n -> p n r"))
         nc.vector.tensor_copy(x_grouped[:, :, 2], x0[:].indirect(offs_sb[:]))
-        for s in range(2):
-            toks = slice(s * HALF, (s + 1) * HALF)
-            entries = slice(s * HALF // LIST_ROWS, (s + 1) * HALF // LIST_ROWS)
-            nc.vector.tensor_copy(x_grouped[:, toks, 3], x3[:].indirect(offs_sb[:, entries]))
-        for s in range(2):
-            toks = slice(s * HALF, (s + 1) * HALF)
+        for t0 in range(0, S, HALF):
+            nc.vector.tensor_copy(x_grouped[:, t0 : t0 + HALF, 3], x3[:].indirect(offs_sb[:, entries(t0, t0 + HALF)]))
+        for t0 in range(0, S, HALF):
             nc.vector.quantize_mx(
-                out=x_codes[:, toks].bitcast(FP8X4),
-                scales=x_scales[:, toks],
-                in_=x_grouped[:, toks, :].rearrange("p n t -> p (n t)"),
+                out=x_codes[:, t0 : t0 + HALF].bitcast(FP8X4),
+                scales=x_scales[:, t0 : t0 + HALF],
+                in_=x_grouped[:, t0 : t0 + HALF, :].rearrange("p n t -> p (n t)"),
             )
 
-        share = 3 * N // 4
-        nc.scalar.copy(w2_bf[:, 0:share], w2[:, 0:share])
-        nc.gpsimd.tensor_copy(w2_bf[:, share:N], w2[:, share:N])
         order = [1, 3, 2, 0]
+        runs_on = [order[0], order[-1]]
+        nc.scalar.copy(w2_bf[:, 0:SCALAR_CAST], w2[:, 0:SCALAR_CAST])
+        nc.gpsimd.tensor_copy(w2_bf[:, SCALAR_CAST:N], w2[:, SCALAR_CAST:N])
         for m in order:
-            words = slice(m * P, (m + 1) * P)
-            entries = slice(m * P // LIST_ROWS, (m + 1) * P // LIST_ROWS)
-            nc.scalar.activation(w_grouped[:, words, 1], w2_bf[:].indirect(pos1_sb[:, entries]), COPY)
+            nc.scalar.activation(
+                w_grouped[:, m * P : (m + 1) * P, 1], w2_bf[:].indirect(pos1_sb[:, entries(m * P, (m + 1) * P)]), COPY
+            )
 
-        def look_up(m):
-            end = (m + 1) * P + (LIST_ROWS if m < 2 else 0)
-            words = slice(m * P, end)
-            entries = slice(m * P // LIST_ROWS, end // LIST_ROWS)
-            nc.vector.tensor_copy(w_grouped[:, words, 3], w3[:].indirect(pos1_sb[:, entries]))
+        def look_up_row_3(m):
+            end = (m + 1) * P + (LIST_ROWS if m in runs_on else 0)
+            nc.vector.tensor_copy(w_grouped[:, m * P : end, 3], w3[:].indirect(pos1_sb[:, entries(m * P, end)]))
 
-        banks = [3, 2, 1, 0, 7, 6, 5, 4, 3, 2, 1, 0]
-        look_up(order[0])
-        look_up(order[1])
+        look_up_row_3(order[0])
+        look_up_row_3(order[1])
+        products = 0
         for i, m in enumerate(order):
             words = slice(m * P, (m + 1) * P)
             nc.vector.quantize_mx(
@@ -116,13 +117,14 @@ def tile_picked_cross_gelu_l_kernel(tc, xT, w, b, offs, pos1, out):
                 in_=w_grouped[:, words, :].rearrange("p n t -> p (n t)"),
             )
             if i + 2 < W_TILES:
-                look_up(order[i + 2])
-            res = keep.tile([P, S], F32, name=f"res{m}", align_bytes=256)
-            cuts = [0, P, HALF, S] if i == 0 else [0, HALF, S]
-            stores = [S] if i == W_TILES - 1 else [HALF, S]
+                look_up_row_3(order[i + 2])
+            cuts = [0, HALF, S]
+            store_ends = [S] if i == W_TILES - 1 else [HALF, S]
+            res = keep.tile([P, S], F32, name=f"res{m}", align_bytes=ALIGN)
             stored = 0
             for c0, c1 in zip(cuts, cuts[1:]):
-                acc = psum.tile([P, HALF], F32, name=f"acc{banks.pop()}")
+                acc = psum.tile([P, HALF], F32, name=f"acc{products % BANKS}")
+                products = products + 1
                 nc.tensor.matmul_mx(
                     out=acc[:, 0 : c1 - c0],
                     lhsT=w_codes[:, words].bitcast(FP8X4),
@@ -132,7 +134,9 @@ def tile_picked_cross_gelu_l_kernel(tc, xT, w, b, offs, pos1, out):
                     start=True,
                     stop=True,
                 )
-                nc.scalar.activation(res[:, c0:c1], acc[:, 0 : c1 - c0], GELU, bias=b_cols[:, m * BLOCK : m * BLOCK + 1])
-                if c1 in stores:
+                nc.scalar.activation(
+                    res[:, c0:c1], acc[:, 0 : c1 - c0], GELU, bias=b_cols[:, m * QUADRANT : m * QUADRANT + 1]
+                )
+                if c1 in store_ends:
                     nc.sync.dma_start(out[words, stored:c1], res[:, stored:c1])
                     stored = c1

@@ -93,31 +93,44 @@ def tile_picked_cross_gelu_l_kernel(tc, xT, w, b, offs, pos1, out):
                 in_=x_grouped[:, t0 : t0 + HALF, :].rearrange("p n t -> p (n t)"),
             )
 
-        order = [1, 3, 2, 0]
-        runs_on = [order[0], order[-1]]
         nc.scalar.copy(w2_bf[:, 0:SCALAR_CAST], w2[:, 0:SCALAR_CAST])
         nc.gpsimd.tensor_copy(w2_bf[:, SCALAR_CAST:N], w2[:, SCALAR_CAST:N])
-        for m in order:
+        for m in range(W_TILES):
             nc.scalar.activation(
                 w_grouped[:, m * P : (m + 1) * P, 1], w2_bf[:].indirect(pos1_sb[:, entries(m * P, (m + 1) * P)]), COPY
             )
 
         def look_up_row_3(m):
-            end = (m + 1) * P + (LIST_ROWS if m in runs_on else 0)
-            nc.vector.tensor_copy(w_grouped[:, m * P : end, 3], w3[:].indirect(pos1_sb[:, entries(m * P, end)]))
+            staged = keep.tile([P, P], BF16, name=f"staged{m}", tag="staged", bufs=2, align_bytes=ALIGN)
+            nc.vector.tensor_copy(staged[:], w3[:].indirect(pos1_sb[:, entries(m * P, (m + 1) * P)]))
+            return staged
 
-        look_up_row_3(order[0])
-        look_up_row_3(order[1])
-        products = 0
-        for i, m in enumerate(order):
+        def put_row_3(m, staged):
+            nc.vector.tensor_copy(w_grouped[:, m * P : (m + 1) * P, 3], staged[:])
+
+        def quantize_words(m):
             words = slice(m * P, (m + 1) * P)
             nc.vector.quantize_mx(
                 out=w_codes[:, words].bitcast(FP8X4),
                 scales=w_scales[:, words],
                 in_=w_grouped[:, words, :].rearrange("p n t -> p (n t)"),
             )
-            if i + 2 < W_TILES:
-                look_up_row_3(order[i + 2])
+
+        nc.vector.tensor_copy(w_grouped[:, 0:P, 3], w3[:].indirect(pos1_sb[:, entries(0, P)]))
+        staged1 = look_up_row_3(1)
+        staged2 = look_up_row_3(2)
+        quantize_words(0)
+        put_row_3(1, staged1)
+        put_row_3(2, staged2)
+        quantize_words(1)
+        staged3 = look_up_row_3(3)
+        quantize_words(2)
+        put_row_3(3, staged3)
+        quantize_words(3)
+
+        products = 0
+        for i, m in enumerate(range(W_TILES)):
+            words = slice(m * P, (m + 1) * P)
             cuts = [0, HALF, S]
             store_ends = [S] if i == W_TILES - 1 else [HALF, S]
             res = keep.tile([P, S], F32, name=f"res{m}", align_bytes=ALIGN)

@@ -67,14 +67,17 @@ def tile_picked_cross_gelu_l_kernel(tc, xT, w, b, offs, pos1, out):
         warm_out = keep.tile([P, 8], F32, name="warm_out")
         nc.scalar.activation(warm_out[:], warm[:], GELU)
 
-        w_grouped = keep.tile([P, V, PACK], BF16, name="w_grouped", align_bytes=ALIGN)
+        first_grouped = keep.tile([P, P, PACK], BF16, name="first_grouped", tag="first", align_bytes=ALIGN)
+        rest_grouped = keep.tile([P, V - P, PACK], BF16, name="rest_grouped", align_bytes=ALIGN)
+        grouped = [first_grouped[:]] + [rest_grouped[:, m * P : (m + 1) * P, :] for m in range(W_TILES - 1)]
         w_codes = keep.tile([P, V], U32, name="w_codes", align_bytes=ALIGN)
         w_scales = keep.tile([P, V], U8, name="w_scales", align_bytes=ALIGN)
         w1_bf = keep.tile([P, N], BF16, name="w1_bf", align_bytes=ALIGN)
         w2_bf = keep.tile([P, N], BF16, name="w2_bf", align_bytes=ALIGN)
         nc.scalar.copy(w1_bf[:], w01[:, 1, :])
-        nc.scalar.activation(w_grouped[:, :, 0], w1_bf[:].indirect(pos1_sb[:]), COPY)
-        nc.vector.tensor_copy(w_grouped[:, :, 2], w01[:, 0, :].indirect(pos1_sb[:]))
+        for part, first, end in ((first_grouped, 0, P), (rest_grouped, P, V)):
+            nc.scalar.activation(part[:, :, 0], w1_bf[:].indirect(pos1_sb[:, entries(first, end)]), COPY)
+            nc.vector.tensor_copy(part[:, :, 2], w01[:, 0, :].indirect(pos1_sb[:, entries(first, end)]))
 
         x_grouped = keep.tile([P, S, PACK], BF16, name="x_grouped", align_bytes=ALIGN)
         x_codes = keep.tile([P, S], U32, name="x_codes", align_bytes=ALIGN)
@@ -96,36 +99,30 @@ def tile_picked_cross_gelu_l_kernel(tc, xT, w, b, offs, pos1, out):
         nc.scalar.copy(w2_bf[:, 0:SCALAR_CAST], w2[:, 0:SCALAR_CAST])
         nc.gpsimd.tensor_copy(w2_bf[:, SCALAR_CAST:N], w2[:, SCALAR_CAST:N])
         for m in range(W_TILES):
-            nc.scalar.activation(
-                w_grouped[:, m * P : (m + 1) * P, 1], w2_bf[:].indirect(pos1_sb[:, entries(m * P, (m + 1) * P)]), COPY
-            )
-
-        def look_up_row_3(m):
-            staged = keep.tile([P, P], BF16, name=f"staged{m}", tag="staged", bufs=2, align_bytes=ALIGN)
-            nc.vector.tensor_copy(staged[:], w3[:].indirect(pos1_sb[:, entries(m * P, (m + 1) * P)]))
-            return staged
-
-        def put_row_3(m, staged):
-            nc.vector.tensor_copy(w_grouped[:, m * P : (m + 1) * P, 3], staged[:])
+            nc.scalar.activation(grouped[m][:, :, 1], w2_bf[:].indirect(pos1_sb[:, entries(m * P, (m + 1) * P)]), COPY)
 
         def quantize_words(m):
             words = slice(m * P, (m + 1) * P)
             nc.vector.quantize_mx(
                 out=w_codes[:, words].bitcast(FP8X4),
                 scales=w_scales[:, words],
-                in_=w_grouped[:, words, :].rearrange("p n t -> p (n t)"),
+                in_=grouped[m].rearrange("p n t -> p (n t)"),
             )
 
-        nc.vector.tensor_copy(w_grouped[:, 0:P, 3], w3[:].indirect(pos1_sb[:, entries(0, P)]))
-        staged1 = look_up_row_3(1)
-        staged2 = look_up_row_3(2)
+        def look_up_row_3(m, dst):
+            nc.vector.tensor_copy(dst, w3[:].indirect(pos1_sb[:, entries(m * P, (m + 1) * P)]))
+
+        look_up_row_3(0, grouped[0][:, :, 3])
+        look_up_row_3(1, grouped[1][:, :, 3])
+        staged2 = keep.tile([P, P], BF16, name="staged2", align_bytes=ALIGN)
+        look_up_row_3(2, staged2[:])
         quantize_words(0)
-        put_row_3(1, staged1)
-        put_row_3(2, staged2)
         quantize_words(1)
-        staged3 = look_up_row_3(3)
+        nc.vector.tensor_copy(grouped[2][:, :, 3], staged2[:])
+        staged3 = keep.tile([P, P], BF16, name="staged3", tag="first", align_bytes=ALIGN)
+        look_up_row_3(3, staged3[:])
         quantize_words(2)
-        put_row_3(3, staged3)
+        nc.vector.tensor_copy(grouped[3][:, :, 3], staged3[:])
         quantize_words(3)
 
         products = 0

@@ -19,8 +19,8 @@ PACK = 4
 LIST_ROWS = 16
 W_TILES = V // P
 HALF = S // 2
+WHOLE_STORE = 1
 QUADRANT = 32
-BANKS = 8
 ALIGN = 256
 SCALAR_CAST = 3 * N // 4
 
@@ -125,28 +125,23 @@ def tile_picked_cross_gelu_l_kernel(tc, xT, w, b, offs, pos1, out):
         nc.vector.tensor_copy(grouped[3][:, :, 3], staged3[:])
         quantize_words(3)
 
-        products = 0
-        for i, m in enumerate(range(W_TILES)):
+        for m in range(W_TILES):
             words = slice(m * P, (m + 1) * P)
-            cuts = [0, HALF, S]
-            store_ends = [S] if i == W_TILES - 1 else [HALF, S]
             res = keep.tile([P, S], F32, name=f"res{m}", align_bytes=ALIGN)
-            stored = 0
-            for c0, c1 in zip(cuts, cuts[1:]):
-                acc = psum.tile([P, HALF], F32, name=f"acc{products % BANKS}")
-                products = products + 1
+            for t0 in range(0, S, HALF):
+                tokens = slice(t0, t0 + HALF)
+                acc = psum.tile([P, HALF], F32, name=f"acc{(m * S + t0) // HALF}")
                 nc.tensor.matmul_mx(
-                    out=acc[:, 0 : c1 - c0],
+                    out=acc[:],
                     lhsT=w_codes[:, words].bitcast(FP8X4),
                     lhsT_scale=w_scales[:, words],
-                    rhs=x_codes[:, c0:c1].bitcast(FP8X4),
-                    rhs_scale=x_scales[:, c0:c1],
+                    rhs=x_codes[:, tokens].bitcast(FP8X4),
+                    rhs_scale=x_scales[:, tokens],
                     start=True,
                     stop=True,
                 )
-                nc.scalar.activation(
-                    res[:, c0:c1], acc[:, 0 : c1 - c0], GELU, bias=b_cols[:, m * QUADRANT : m * QUADRANT + 1]
-                )
-                if c1 in store_ends:
-                    nc.sync.dma_start(out[words, stored:c1], res[:, stored:c1])
-                    stored = c1
+                nc.scalar.activation(res[:, tokens], acc[:], GELU, bias=b_cols[:, m * QUADRANT : m * QUADRANT + 1])
+                if m != WHOLE_STORE:
+                    nc.sync.dma_start(out[words, tokens], res[:, tokens])
+            if m == WHOLE_STORE:
+                nc.sync.dma_start(out[words, :], res[:])

@@ -19,10 +19,10 @@ PACK = 4
 LIST_ROWS = 16
 W_TILES = V // P
 HALF = S // 2
-WHOLE_STORE = 1
 QUADRANT = 32
 ALIGN = 256
 SCALAR_CAST = 3 * N // 4
+WHOLE_STORE = 1
 
 
 def tile_picked_cross_gelu_l_kernel(tc, xT, w, b, offs, pos1, out):
@@ -37,16 +37,14 @@ def tile_picked_cross_gelu_l_kernel(tc, xT, w, b, offs, pos1, out):
         keep = ctx.enter_context(tc.tile_pool(name="keep", bufs=1))
         psum = ctx.enter_context(tc.psum_pool(name="psum", bufs=1))
 
-        pos1_sb = keep.tile([P, V // LIST_ROWS], U16, name="pos1_sb", align_bytes=ALIGN)
-        offs_sb = keep.tile([P, S // LIST_ROWS], U16, name="offs_sb", align_bytes=ALIGN)
-        w01 = keep.tile([P, 2, N], F32, name="w01", align_bytes=ALIGN)
-        w2 = keep.tile([P, N], F32, name="w2", align_bytes=ALIGN)
-        w3 = keep.tile([P, N], F32, name="w3", align_bytes=ALIGN)
-        x12 = keep.tile([P, 2, T], F32, name="x12", align_bytes=ALIGN)
-        x0 = keep.tile([P, T], F32, name="x0", align_bytes=ALIGN)
-        x3 = keep.tile([P, T], F32, name="x3", align_bytes=ALIGN)
-        b_rows = keep.tile([P, P], F32, name="b_rows", align_bytes=ALIGN)
-        b_cols = keep.tile([P, P], F32, name="b_cols", align_bytes=ALIGN)
+        def sb(name, shape, dtype):
+            return keep.tile(shape, dtype, name=name, align_bytes=ALIGN)
+
+        pos1_sb = sb("pos1_sb", [P, V // LIST_ROWS], U16)
+        offs_sb = sb("offs_sb", [P, S // LIST_ROWS], U16)
+        w01, w2, w3 = sb("w01", [P, 2, N], F32), sb("w2", [P, N], F32), sb("w3", [P, N], F32)
+        x12, x0, x3 = sb("x12", [P, 2, T], F32), sb("x0", [P, T], F32), sb("x3", [P, T], F32)
+        b_rows, b_cols = sb("b_rows", [P, P], F32), sb("b_cols", [P, P], F32)
         nc.gpsimd.memset(b_rows[:], 0.0)
         nc.scalar.dma_start(w01[:], w_rows[:, 0:2, :])
         nc.scalar.dma_start(
@@ -67,67 +65,66 @@ def tile_picked_cross_gelu_l_kernel(tc, xT, w, b, offs, pos1, out):
         warm_out = keep.tile([P, 8], F32, name="warm_out")
         nc.scalar.activation(warm_out[:], warm[:], GELU)
 
-        first_grouped = keep.tile([P, P, PACK], BF16, name="first_grouped", tag="first", align_bytes=ALIGN)
-        rest_grouped = keep.tile([P, V - P, PACK], BF16, name="rest_grouped", align_bytes=ALIGN)
-        grouped = [first_grouped[:]] + [rest_grouped[:, m * P : (m + 1) * P, :] for m in range(W_TILES - 1)]
-        w_codes = keep.tile([P, V], U32, name="w_codes", align_bytes=ALIGN)
-        w_scales = keep.tile([P, V], U8, name="w_scales", align_bytes=ALIGN)
-        w1_bf = keep.tile([P, N], BF16, name="w1_bf", align_bytes=ALIGN)
-        w2_bf = keep.tile([P, N], BF16, name="w2_bf", align_bytes=ALIGN)
-        nc.scalar.copy(w1_bf[:], w01[:, 1, :])
-        for part, first, end in ((first_grouped, 0, P), (rest_grouped, P, V)):
-            nc.scalar.activation(part[:, :, 0], w1_bf[:].indirect(pos1_sb[:, entries(first, end)]), COPY)
-            nc.vector.tensor_copy(part[:, :, 2], w01[:, 0, :].indirect(pos1_sb[:, entries(first, end)]))
+        w_codes, w_scales = sb("w_codes", [P, V], U32), sb("w_scales", [P, V], U8)
+        x_codes, x_scales = sb("x_codes", [P, S], U32), sb("x_scales", [P, S], U8)
+        w1_bf, w2_bf = sb("w1_bf", [P, N], BF16), sb("w2_bf", [P, N], BF16)
+        first = sb("first", [P, P + P * PACK], BF16)
+        rest_grouped = sb("rest_grouped", [P, V - P, PACK], BF16)
+        grouped = [first[:, P:].rearrange("p (n t) -> p n t", t=PACK)]
+        grouped = grouped + [rest_grouped[:, m * P : (m + 1) * P, :] for m in range(W_TILES - 1)]
+        x_grouped = sb("x_grouped", [P, S, PACK], BF16)
 
-        x_grouped = keep.tile([P, S, PACK], BF16, name="x_grouped", align_bytes=ALIGN)
-        x_codes = keep.tile([P, S], U32, name="x_codes", align_bytes=ALIGN)
-        x_scales = keep.tile([P, S], U8, name="x_scales", align_bytes=ALIGN)
-        x12_picked = keep.tile([P, 2, S], F32, name="x12_picked", align_bytes=ALIGN)
+        def words_of(first_tile, end_tile):
+            return pos1_sb[:, entries(first_tile * P, end_tile * P)]
+
+        def quantize(codes, scales, cols, src):
+            nc.vector.quantize_mx(out=codes[:, cols].bitcast(FP8X4), scales=scales[:, cols], in_=src.rearrange("p n t -> p (n t)"))
+
+        def quantize_words(m):
+            quantize(w_codes, w_scales, slice(m * P, (m + 1) * P), grouped[m])
+
+        nc.scalar.copy(w1_bf[:], w01[:, 1, :])
+        for part, lo, hi in ((grouped[0], 0, 1), (rest_grouped[:], 1, W_TILES)):
+            nc.scalar.activation(part[:, :, 0], w1_bf[:].indirect(words_of(lo, hi)), COPY)
+            nc.vector.tensor_copy(part[:, :, 2], w01[:, 0, :].indirect(words_of(lo, hi)))
+
+        x12_picked = sb("x12_picked", [P, 2, S], F32)
         for r in range(2):
             nc.vector.tensor_copy(x12_picked[:, r, :], x12[:, r, :].indirect(offs_sb[:]))
         nc.scalar.copy(x_grouped[:, :, 0:2], x12_picked[:].rearrange("p r n -> p n r"))
         nc.vector.tensor_copy(x_grouped[:, :, 2], x0[:].indirect(offs_sb[:]))
         for t0 in range(0, S, HALF):
             nc.vector.tensor_copy(x_grouped[:, t0 : t0 + HALF, 3], x3[:].indirect(offs_sb[:, entries(t0, t0 + HALF)]))
+
         for t0 in range(0, S, HALF):
-            nc.vector.quantize_mx(
-                out=x_codes[:, t0 : t0 + HALF].bitcast(FP8X4),
-                scales=x_scales[:, t0 : t0 + HALF],
-                in_=x_grouped[:, t0 : t0 + HALF, :].rearrange("p n t -> p (n t)"),
-            )
+            quantize(x_codes, x_scales, slice(t0, t0 + HALF), x_grouped[:, t0 : t0 + HALF, :])
 
         nc.scalar.copy(w2_bf[:, 0:SCALAR_CAST], w2[:, 0:SCALAR_CAST])
         nc.gpsimd.tensor_copy(w2_bf[:, SCALAR_CAST:N], w2[:, SCALAR_CAST:N])
-        for m in range(W_TILES):
-            nc.scalar.activation(grouped[m][:, :, 1], w2_bf[:].indirect(pos1_sb[:, entries(m * P, (m + 1) * P)]), COPY)
 
-        def quantize_words(m):
-            words = slice(m * P, (m + 1) * P)
-            nc.vector.quantize_mx(
-                out=w_codes[:, words].bitcast(FP8X4),
-                scales=w_scales[:, words],
-                in_=grouped[m].rearrange("p n t -> p (n t)"),
-            )
+        late2 = sb("late2", [P, 2, P], BF16)
+        for m in range(2):
+            nc.scalar.activation(grouped[m][:, :, 1], w2_bf[:].indirect(words_of(m, m + 1)), COPY)
+        nc.scalar.activation(late2[:, 0, :], w2_bf[:].indirect(words_of(2, 3)), COPY)
+        nc.scalar.activation(first[:, 0:P], w2_bf[:].indirect(words_of(3, 4)), COPY)
 
-        def look_up_row_3(m, dst):
-            nc.vector.tensor_copy(dst, w3[:].indirect(pos1_sb[:, entries(m * P, (m + 1) * P)]))
+        def put(m, planes):
+            nc.vector.tensor_copy(grouped[m][:, :, 1:PACK:2], planes.rearrange("p r n -> p n r"))
 
-        look_up_row_3(0, grouped[0][:, :, 3])
-        look_up_row_3(1, grouped[1][:, :, 3])
-        staged2 = keep.tile([P, P], BF16, name="staged2", align_bytes=ALIGN)
-        look_up_row_3(2, staged2[:])
+        for m in range(2):
+            nc.vector.tensor_copy(grouped[m][:, :, 3], w3[:].indirect(words_of(m, m + 1)))
+        nc.vector.tensor_copy(late2[:, 1, :], w3[:].indirect(words_of(2, 3)))
         quantize_words(0)
         quantize_words(1)
-        nc.vector.tensor_copy(grouped[2][:, :, 3], staged2[:])
-        staged3 = keep.tile([P, P], BF16, name="staged3", tag="first", align_bytes=ALIGN)
-        look_up_row_3(3, staged3[:])
+        put(2, late2[:])
+        nc.vector.tensor_copy(first[:, P : 2 * P], w3[:].indirect(words_of(3, 4)))
         quantize_words(2)
-        nc.vector.tensor_copy(grouped[3][:, :, 3], staged3[:])
+        put(3, first[:, 0 : 2 * P].rearrange("p (r n) -> p r n", r=2))
         quantize_words(3)
 
         for m in range(W_TILES):
             words = slice(m * P, (m + 1) * P)
-            res = keep.tile([P, S], F32, name=f"res{m}", align_bytes=ALIGN)
+            res = sb(f"res{m}", [P, S], F32)
             for t0 in range(0, S, HALF):
                 tokens = slice(t0, t0 + HALF)
                 acc = psum.tile([P, HALF], F32, name=f"acc{(m * S + t0) // HALF}")

@@ -119,8 +119,11 @@ def tile_picked_cross_gelu_l_kernel(tc, xT, w, b, offs, pos1, out):
         put(2, late2[:])
         nc.vector.tensor_copy(first[:, P : 2 * P], w3[:].indirect(words_of(3, 4)))
         quantize_words(2)
-        put(3, first[:, 0 : 2 * P].rearrange("p (r n) -> p r n", r=2))
-        quantize_words(3)
+        late3 = first[:, 0 : 2 * P].rearrange("p (r n) -> p n r", r=2)
+        for n0 in range(0, P, P // 2):
+            nc.vector.tensor_copy(grouped[3][:, n0 : n0 + P // 2, 1:PACK:2], late3[:, n0 : n0 + P // 2, :])
+        for n0 in range(0, P, P // 2):
+            quantize(w_codes, w_scales, slice(3 * P + n0, 3 * P + n0 + P // 2), grouped[3][:, n0 : n0 + P // 2, :])
 
         for m in range(W_TILES):
             words = slice(m * P, (m + 1) * P)

@@ -21,17 +21,13 @@ W_TILES = V // P
 HALF = S // 2
 QUADRANT = 32
 ALIGN = 256
-SCALAR_CAST = 3 * N // 4
-WHOLE_STORE = 1
+BANKS = 8
 
 
 def tile_picked_cross_gelu_l_kernel(tc, xT, w, b, offs, pos1, out):
     nc = tc.nc
-    x_rows = xT.rearrange("(p r) c -> p r c", r=PACK)
-    w_rows = w.rearrange("(p r) c -> p r c", r=PACK)
-
-    def entries(first, end):
-        return slice(first // LIST_ROWS, end // LIST_ROWS)
+    x_rows = xT.rearrange("(p r) c -> p (r c)", r=PACK)
+    w_rows = w.rearrange("(p r) c -> p (r c)", r=PACK)
 
     with ExitStack() as ctx:
         keep = ctx.enter_context(tc.tile_pool(name="keep", bufs=1))
@@ -42,22 +38,21 @@ def tile_picked_cross_gelu_l_kernel(tc, xT, w, b, offs, pos1, out):
 
         pos1_sb = sb("pos1_sb", [P, V // LIST_ROWS], U16)
         offs_sb = sb("offs_sb", [P, S // LIST_ROWS], U16)
-        w01, w2, w3 = sb("w01", [P, 2, N], F32), sb("w2", [P, N], F32), sb("w3", [P, N], F32)
-        x12, x0, x3 = sb("x12", [P, 2, T], F32), sb("x0", [P, T], F32), sb("x3", [P, T], F32)
+        w01, w23 = sb("w01", [P, 2 * N], F32), sb("w23", [P, 2 * N], F32)
+        x01, x2, x3 = sb("x01", [P, 2 * T], F32), sb("x2", [P, T], F32), sb("x3", [P, T], F32)
         b_rows, b_cols = sb("b_rows", [P, P], F32), sb("b_cols", [P, P], F32)
         nc.gpsimd.memset(b_rows[:], 0.0)
-        nc.scalar.dma_start(w01[:], w_rows[:, 0:2, :])
+        nc.scalar.dma_start(w01[:], w_rows[:, 0 : 2 * N])
         nc.scalar.dma_start(
             b_rows[0:P:QUADRANT, :].rearrange("q (m j) -> q m j", j=QUADRANT),
             b.rearrange("(m q j) o -> q m (j o)", m=W_TILES, j=QUADRANT),
         )
         nc.sync.dma_start(pos1_sb[:], pos1)
         nc.sync.dma_start(offs_sb[:], offs)
-        nc.sync.dma_start(x12[:], x_rows[:, 1:3, :])
-        nc.sync.dma_start(x0[:], x_rows[:, 0, :])
-        nc.sync.dma_start(x3[:], x_rows[:, 3, :])
-        nc.sync.dma_start(w2[:], w_rows[:, 2, :])
-        nc.sync.dma_start(w3[:], w_rows[:, 3, :])
+        nc.sync.dma_start(w23[:], w_rows[:, 2 * N : 4 * N])
+        nc.sync.dma_start(x01[:], x_rows[:, 0 : 2 * T])
+        nc.sync.dma_start(x3[:], x_rows[:, 3 * T : 4 * T])
+        nc.sync.dma_start(x2[:], x_rows[:, 2 * T : 3 * T])
         nc.vector.transpose(b_cols[:], b_rows[:])
 
         warm = keep.tile([P, 8], F32, name="warm")
@@ -67,81 +62,55 @@ def tile_picked_cross_gelu_l_kernel(tc, xT, w, b, offs, pos1, out):
 
         w_codes, w_scales = sb("w_codes", [P, V], U32), sb("w_scales", [P, V], U8)
         x_codes, x_scales = sb("x_codes", [P, S], U32), sb("x_scales", [P, S], U8)
-        w1_bf, w2_bf = sb("w1_bf", [P, N], BF16), sb("w2_bf", [P, N], BF16)
-        first = sb("first", [P, P + P * PACK], BF16)
-        rest_grouped = sb("rest_grouped", [P, V - P, PACK], BF16)
-        grouped = [first[:, P:].rearrange("p (n t) -> p n t", t=PACK)]
-        grouped = grouped + [rest_grouped[:, m * P : (m + 1) * P, :] for m in range(W_TILES - 1)]
+        w_grouped = sb("w_grouped", [P, V, PACK], BF16)
         x_grouped = sb("x_grouped", [P, S, PACK], BF16)
+        staged = sb("staged", [P, 2, P], BF16)
 
-        def words_of(first_tile, end_tile):
-            return pos1_sb[:, entries(first_tile * P, end_tile * P)]
+        def tokens_of(first, end):
+            return offs_sb[:, first // LIST_ROWS : end // LIST_ROWS]
 
-        def quantize(codes, scales, cols, src):
-            nc.vector.quantize_mx(out=codes[:, cols].bitcast(FP8X4), scales=scales[:, cols], in_=src.rearrange("p n t -> p (n t)"))
+        def quantize(codes, scales, grouped, first, end):
+            nc.vector.quantize_mx(
+                out=codes[:, first:end].bitcast(FP8X4),
+                scales=scales[:, first:end],
+                in_=grouped[:, first:end, :].rearrange("p n t -> p (n t)"),
+            )
 
-        def quantize_words(m):
-            quantize(w_codes, w_scales, slice(m * P, (m + 1) * P), grouped[m])
+        nc.scalar.activation(w_grouped[:, :, 0], w01[:].indirect(pos1_sb[:]), COPY)
+        nc.vector.tensor_copy(w_grouped[:, :, 2], w01[:, N : 2 * N].indirect(pos1_sb[:]))
+        nc.scalar.activation(w_grouped[:, :, 1], w23[:].indirect(pos1_sb[:]), COPY)
+        nc.vector.tensor_copy(w_grouped[:, :, 3], w23[:, N : 2 * N].indirect(pos1_sb[:]))
+        quantize(w_codes, w_scales, w_grouped, 0, V)
 
-        nc.scalar.copy(w1_bf[:], w01[:, 1, :])
-        for part, lo, hi in ((grouped[0], 0, 1), (rest_grouped[:], 1, W_TILES)):
-            nc.scalar.activation(part[:, :, 0], w1_bf[:].indirect(words_of(lo, hi)), COPY)
-            nc.vector.tensor_copy(part[:, :, 2], w01[:, 0, :].indirect(words_of(lo, hi)))
+        def shared_row(place, window):
+            nc.vector.tensor_copy(staged[:, place, :], window.indirect(tokens_of(S - P, S)))
+            for first in range(0, S - P, P):
+                nc.scalar.activation(x_grouped[:, first : first + P, place], window.indirect(tokens_of(first, first + P)), COPY)
 
-        x12_picked = sb("x12_picked", [P, 2, S], F32)
-        for r in range(2):
-            nc.vector.tensor_copy(x12_picked[:, r, :], x12[:, r, :].indirect(offs_sb[:]))
-        nc.scalar.copy(x_grouped[:, :, 0:2], x12_picked[:].rearrange("p r n -> p n r"))
-        nc.vector.tensor_copy(x_grouped[:, :, 2], x0[:].indirect(offs_sb[:]))
-        for t0 in range(0, S, HALF):
-            nc.vector.tensor_copy(x_grouped[:, t0 : t0 + HALF, 3], x3[:].indirect(offs_sb[:, entries(t0, t0 + HALF)]))
+        shared_row(0, x01[:])
+        nc.vector.tensor_copy(x_grouped[:, :, 2], x01[:, T : 2 * T].indirect(offs_sb[:]))
+        nc.vector.tensor_copy(x_grouped[:, :, 3], x3[:].indirect(offs_sb[:]))
+        shared_row(1, x2[:])
+        quantize(x_codes, x_scales, x_grouped, 0, P)
+        nc.vector.tensor_copy(x_grouped[:, S - P : S, 0:2], staged[:].rearrange("p r n -> p n r"))
+        quantize(x_codes, x_scales, x_grouped, P, HALF)
+        quantize(x_codes, x_scales, x_grouped, HALF, S)
 
-        for t0 in range(0, S, HALF):
-            quantize(x_codes, x_scales, slice(t0, t0 + HALF), x_grouped[:, t0 : t0 + HALF, :])
-
-        nc.scalar.copy(w2_bf[:, 0:SCALAR_CAST], w2[:, 0:SCALAR_CAST])
-        nc.gpsimd.tensor_copy(w2_bf[:, SCALAR_CAST:N], w2[:, SCALAR_CAST:N])
-
-        late2 = sb("late2", [P, 2, P], BF16)
-        for m in range(2):
-            nc.scalar.activation(grouped[m][:, :, 1], w2_bf[:].indirect(words_of(m, m + 1)), COPY)
-        nc.scalar.activation(late2[:, 0, :], w2_bf[:].indirect(words_of(2, 3)), COPY)
-        nc.scalar.activation(first[:, 0:P], w2_bf[:].indirect(words_of(3, 4)), COPY)
-
-        def put(m, planes):
-            nc.vector.tensor_copy(grouped[m][:, :, 1:PACK:2], planes.rearrange("p r n -> p n r"))
-
-        for m in range(2):
-            nc.vector.tensor_copy(grouped[m][:, :, 3], w3[:].indirect(words_of(m, m + 1)))
-        nc.vector.tensor_copy(late2[:, 1, :], w3[:].indirect(words_of(2, 3)))
-        quantize_words(0)
-        quantize_words(1)
-        put(2, late2[:])
-        nc.vector.tensor_copy(first[:, P : 2 * P], w3[:].indirect(words_of(3, 4)))
-        quantize_words(2)
-        late3 = first[:, 0 : 2 * P].rearrange("p (r n) -> p n r", r=2)
-        for n0 in range(0, P, P // 2):
-            nc.vector.tensor_copy(grouped[3][:, n0 : n0 + P // 2, 1:PACK:2], late3[:, n0 : n0 + P // 2, :])
-        for n0 in range(0, P, P // 2):
-            quantize(w_codes, w_scales, slice(3 * P + n0, 3 * P + n0 + P // 2), grouped[3][:, n0 : n0 + P // 2, :])
-
-        for m in range(W_TILES):
-            words = slice(m * P, (m + 1) * P)
-            res = sb(f"res{m}", [P, S], F32)
-            for t0 in range(0, S, HALF):
-                tokens = slice(t0, t0 + HALF)
-                acc = psum.tile([P, HALF], F32, name=f"acc{(m * S + t0) // HALF}")
-                nc.tensor.matmul_mx(
-                    out=acc[:],
-                    lhsT=w_codes[:, words].bitcast(FP8X4),
-                    lhsT_scale=w_scales[:, words],
-                    rhs=x_codes[:, tokens].bitcast(FP8X4),
-                    rhs_scale=x_scales[:, tokens],
-                    start=True,
-                    stop=True,
-                )
-                nc.scalar.activation(res[:, tokens], acc[:], GELU, bias=b_cols[:, m * QUADRANT : m * QUADRANT + 1])
-                if m != WHOLE_STORE:
-                    nc.sync.dma_start(out[words, tokens], res[:, tokens])
-            if m == WHOLE_STORE:
-                nc.sync.dma_start(out[words, :], res[:])
+        res = [sb(f"res{m}", [P, S], F32) for m in range(W_TILES)]
+        pieces = [(0, 0, P), (0, P, HALF)]
+        pieces = pieces + [(m, 0, HALF) for m in range(1, W_TILES)] + [(m, HALF, S) for m in range(W_TILES)]
+        for i, (m, first, end) in enumerate(pieces):
+            words, tokens = slice(m * P, (m + 1) * P), slice(first, end)
+            acc = psum.tile([P, HALF], F32, name=f"acc{i % BANKS}")
+            nc.tensor.matmul_mx(
+                out=acc[:, 0 : end - first],
+                lhsT=w_codes[:, words].bitcast(FP8X4),
+                lhsT_scale=w_scales[:, words],
+                rhs=x_codes[:, tokens].bitcast(FP8X4),
+                rhs_scale=x_scales[:, tokens],
+                start=True,
+                stop=True,
+            )
+            nc.scalar.activation(res[m][:, tokens], acc[:, 0 : end - first], GELU, bias=b_cols[:, m * QUADRANT : m * QUADRANT + 1])
+            if end % HALF == 0:
+                nc.sync.dma_start(out[words, end - HALF : end], res[m][:, end - HALF : end])

@@ -88,8 +88,12 @@ def tile_picked_cross_gelu_l_kernel(tc, xT, w, b, offs, pos1, out):
                 nc.scalar.activation(x_grouped[:, first : first + P, place], window.indirect(tokens_of(first, first + P)), COPY)
 
         shared_row(0, x01[:])
-        nc.vector.tensor_copy(x_grouped[:, :, 2], x01[:, T : 2 * T].indirect(offs_sb[:]))
-        nc.vector.tensor_copy(x_grouped[:, :, 3], x3[:].indirect(offs_sb[:]))
+        x1_picked = sb("x1_picked", [P, HALF], F32)
+        nc.vector.tensor_copy(x1_picked[:], x01[:, T : 2 * T].indirect(tokens_of(0, HALF)))
+        nc.vector.tensor_copy(x_grouped[:, HALF:S, 2], x01[:, T : 2 * T].indirect(tokens_of(HALF, S)))
+        nc.scalar.copy(x_grouped[:, 0:HALF, 2], x1_picked[:])
+        nc.scalar.activation(x_grouped[:, 0:HALF, 3], x3[:].indirect(tokens_of(0, HALF)), COPY)
+        nc.vector.tensor_copy(x_grouped[:, HALF:S, 3], x3[:].indirect(tokens_of(HALF, S)))
         shared_row(1, x2[:])
         quantize(x_codes, x_scales, x_grouped, 0, P)
         nc.vector.tensor_copy(x_grouped[:, S - P : S, 0:2], staged[:].rearrange("p r n -> p n r"))

@@ -38,21 +38,21 @@ def tile_picked_cross_gelu_l_kernel(tc, xT, w, b, offs, pos1, out):
 
         pos1_sb = sb("pos1_sb", [P, V // LIST_ROWS], U16)
         offs_sb = sb("offs_sb", [P, S // LIST_ROWS], U16)
-        w01, w23 = sb("w01", [P, 2 * N], F32), sb("w23", [P, 2 * N], F32)
+        w012, w3 = sb("w012", [P, 3 * N], F32), sb("w3", [P, N], F32)
         x01, x2, x3 = sb("x01", [P, 2 * T], F32), sb("x2", [P, T], F32), sb("x3", [P, T], F32)
         b_rows, b_cols = sb("b_rows", [P, P], F32), sb("b_cols", [P, P], F32)
         nc.gpsimd.memset(b_rows[:], 0.0)
-        nc.scalar.dma_start(w01[:], w_rows[:, 0 : 2 * N])
+        nc.scalar.dma_start(w012[:], w_rows[:, 0 : 3 * N])
         nc.scalar.dma_start(
             b_rows[0:P:QUADRANT, :].rearrange("q (m j) -> q m j", j=QUADRANT),
             b.rearrange("(m q j) o -> q m (j o)", m=W_TILES, j=QUADRANT),
         )
         nc.sync.dma_start(pos1_sb[:], pos1)
         nc.sync.dma_start(offs_sb[:], offs)
-        nc.sync.dma_start(w23[:], w_rows[:, 2 * N : 4 * N])
         nc.sync.dma_start(x01[:], x_rows[:, 0 : 2 * T])
-        nc.sync.dma_start(x3[:], x_rows[:, 3 * T : 4 * T])
         nc.sync.dma_start(x2[:], x_rows[:, 2 * T : 3 * T])
+        nc.sync.dma_start(x3[:], x_rows[:, 3 * T : 4 * T])
+        nc.sync.dma_start(w3[:], w_rows[:, 3 * N : 4 * N])
         nc.vector.transpose(b_cols[:], b_rows[:])
 
         warm = keep.tile([P, 8], F32, name="warm")
@@ -62,12 +62,17 @@ def tile_picked_cross_gelu_l_kernel(tc, xT, w, b, offs, pos1, out):
 
         w_codes, w_scales = sb("w_codes", [P, V], U32), sb("w_scales", [P, V], U8)
         x_codes, x_scales = sb("x_codes", [P, S], U32), sb("x_scales", [P, S], U8)
-        w_grouped = sb("w_grouped", [P, V, PACK], BF16)
+        w_work = sb("w_work", [P, P + V * PACK], BF16)
+        w_grouped = w_work[:, P:].rearrange("p (n t) -> p n t", t=PACK)
         x_grouped = sb("x_grouped", [P, S, PACK], BF16)
-        staged = sb("staged", [P, 2, P], BF16)
+        x1_picked = sb("x1_picked", [P, HALF], F32)
+        last = V - P
 
         def tokens_of(first, end):
             return offs_sb[:, first // LIST_ROWS : end // LIST_ROWS]
+
+        def words_of(first, end):
+            return pos1_sb[:, first // LIST_ROWS : end // LIST_ROWS]
 
         def quantize(codes, scales, grouped, first, end):
             nc.vector.quantize_mx(
@@ -76,45 +81,47 @@ def tile_picked_cross_gelu_l_kernel(tc, xT, w, b, offs, pos1, out):
                 in_=grouped[:, first:end, :].rearrange("p n t -> p (n t)"),
             )
 
-        nc.scalar.activation(w_grouped[:, :, 0], w01[:].indirect(pos1_sb[:]), COPY)
-        nc.vector.tensor_copy(w_grouped[:, :, 2], w01[:, N : 2 * N].indirect(pos1_sb[:]))
-        nc.scalar.activation(w_grouped[:, :, 1], w23[:].indirect(pos1_sb[:]), COPY)
-        nc.vector.tensor_copy(w_grouped[:, :, 3], w23[:, N : 2 * N].indirect(pos1_sb[:]))
-        quantize(w_codes, w_scales, w_grouped, 0, V)
+        nc.scalar.activation(w_grouped[:, 0:last, 0], w012[:].indirect(words_of(0, last)), COPY)
+        nc.scalar.activation(w_work[:, 0:P], w012[:].indirect(words_of(last, V)), COPY)
+        nc.vector.tensor_copy(w_grouped[:, :, 2], w012[:, N : 2 * N].indirect(pos1_sb[:]))
+        nc.vector.tensor_copy(w_grouped[:, :, 3], w012[:, 2 * N : 3 * N].indirect(pos1_sb[:]))
 
-        def shared_row(place, window):
-            nc.vector.tensor_copy(staged[:, place, :], window.indirect(tokens_of(S - P, S)))
-            for first in range(0, S - P, P):
-                nc.scalar.activation(x_grouped[:, first : first + P, place], window.indirect(tokens_of(first, first + P)), COPY)
+        def shared_row(place, tile):
+            nc.scalar.activation(x_grouped[:, 0:HALF, place], tile[:].indirect(tokens_of(0, HALF)), COPY)
+            nc.vector.tensor_copy(x_grouped[:, HALF:S, place], tile[:, 0:T].indirect(tokens_of(HALF, S)))
 
-        shared_row(0, x01[:])
-        x1_picked = sb("x1_picked", [P, HALF], F32)
         nc.vector.tensor_copy(x1_picked[:], x01[:, T : 2 * T].indirect(tokens_of(0, HALF)))
+        shared_row(0, x01)
         nc.vector.tensor_copy(x_grouped[:, HALF:S, 2], x01[:, T : 2 * T].indirect(tokens_of(HALF, S)))
         nc.scalar.copy(x_grouped[:, 0:HALF, 2], x1_picked[:])
-        nc.scalar.activation(x_grouped[:, 0:HALF, 3], x3[:].indirect(tokens_of(0, HALF)), COPY)
-        nc.vector.tensor_copy(x_grouped[:, HALF:S, 3], x3[:].indirect(tokens_of(HALF, S)))
-        shared_row(1, x2[:])
-        quantize(x_codes, x_scales, x_grouped, 0, P)
-        nc.vector.tensor_copy(x_grouped[:, S - P : S, 0:2], staged[:].rearrange("p r n -> p n r"))
-        quantize(x_codes, x_scales, x_grouped, P, HALF)
+        shared_row(3, x2)
+        shared_row(1, x3)
         quantize(x_codes, x_scales, x_grouped, HALF, S)
+        quantize(x_codes, x_scales, x_grouped, 0, HALF)
 
-        res = [sb(f"res{m}", [P, S], F32) for m in range(W_TILES)]
-        pieces = [(0, 0, P), (0, P, HALF)]
-        pieces = pieces + [(m, 0, HALF) for m in range(1, W_TILES)] + [(m, HALF, S) for m in range(W_TILES)]
-        for i, (m, first, end) in enumerate(pieces):
-            words, tokens = slice(m * P, (m + 1) * P), slice(first, end)
-            acc = psum.tile([P, HALF], F32, name=f"acc{i % BANKS}")
-            nc.tensor.matmul_mx(
-                out=acc[:, 0 : end - first],
-                lhsT=w_codes[:, words].bitcast(FP8X4),
-                lhsT_scale=w_scales[:, words],
-                rhs=x_codes[:, tokens].bitcast(FP8X4),
-                rhs_scale=x_scales[:, tokens],
-                start=True,
-                stop=True,
-            )
-            nc.scalar.activation(res[m][:, tokens], acc[:, 0 : end - first], GELU, bias=b_cols[:, m * QUADRANT : m * QUADRANT + 1])
-            if end % HALF == 0:
-                nc.sync.dma_start(out[words, end - HALF : end], res[m][:, end - HALF : end])
+        for first in range(0, last, P):
+            nc.scalar.activation(w_grouped[:, first : first + P, 1], w3[:].indirect(words_of(first, first + P)), COPY)
+        quantize(w_codes, w_scales, w_grouped, 0, P)
+        nc.vector.tensor_copy(w_work[:, P : 2 * P], w3[:].indirect(words_of(last, V)))
+        quantize(w_codes, w_scales, w_grouped, P, 2 * P)
+        nc.vector.tensor_copy(w_grouped[:, last:V, 0:2], w_work[:, 0 : 2 * P].rearrange("p (r n) -> p n r", r=2))
+        quantize(w_codes, w_scales, w_grouped, 2 * P, last)
+        quantize(w_codes, w_scales, w_grouped, last, V)
+
+        for m in range(W_TILES):
+            words = slice(m * P, (m + 1) * P)
+            res = sb(f"res{m}", [P, S], F32)
+            for first in range(0, S, HALF):
+                tokens = slice(first, first + HALF)
+                acc = psum.tile([P, HALF], F32, name=f"acc{(m * S + first) // HALF}")
+                nc.tensor.matmul_mx(
+                    out=acc[:],
+                    lhsT=w_codes[:, words].bitcast(FP8X4),
+                    lhsT_scale=w_scales[:, words],
+                    rhs=x_codes[:, tokens].bitcast(FP8X4),
+                    rhs_scale=x_scales[:, tokens],
+                    start=True,
+                    stop=True,
+                )
+                nc.scalar.activation(res[:, tokens], acc[:], GELU, bias=b_cols[:, m * QUADRANT : m * QUADRANT + 1])
+                nc.sync.dma_start(out[words, tokens], res[:, tokens])

@@ -22,6 +22,7 @@ HALF = S // 2
 QUADRANT = 32
 ALIGN = 256
 BANKS = 8
+EDGE = 64
 
 
 def tile_picked_cross_gelu_l_kernel(tc, xT, w, b, offs, pos1, out):
@@ -31,6 +32,7 @@ def tile_picked_cross_gelu_l_kernel(tc, xT, w, b, offs, pos1, out):
 
     with ExitStack() as ctx:
         keep = ctx.enter_context(tc.tile_pool(name="keep", bufs=1))
+        reuse = ctx.enter_context(tc.tile_pool(name="reuse", bufs=1))
         psum = ctx.enter_context(tc.psum_pool(name="psum", bufs=1))
 
         def sb(name, shape, dtype):
@@ -61,10 +63,12 @@ def tile_picked_cross_gelu_l_kernel(tc, xT, w, b, offs, pos1, out):
         nc.scalar.activation(warm_out[:], warm[:], GELU)
 
         w_codes, w_scales = sb("w_codes", [P, V], U32), sb("w_scales", [P, V], U8)
-        x_codes, x_scales = sb("x_codes", [P, S], U32), sb("x_scales", [P, S], U8)
-        w_work = sb("w_work", [P, P + V * PACK], BF16)
-        w_grouped = w_work[:, P:].rearrange("p (n t) -> p n t", t=PACK)
-        x_grouped = sb("x_grouped", [P, S, PACK], BF16)
+        x_codes = sb("x_codes", [P, S], U32)
+        w_work = sb("w_work", [P, V * PACK + 2 * P], BF16)
+        w_grouped = w_work[:, 0 : V * PACK].rearrange("p (n t) -> p n t", t=PACK)
+        staged = w_work[:, V * PACK - P : V * PACK - P + 2 * P].rearrange("p (r n) -> p r n", r=2)
+        x_head = reuse.tile([P, P, PACK], BF16, name="x_head", align_bytes=ALIGN, offset=0)
+        x_rest = sb("x_rest", [P, S - P, PACK], BF16)
         x1_picked = sb("x1_picked", [P, HALF], F32)
         last = V - P
 
@@ -74,54 +78,65 @@ def tile_picked_cross_gelu_l_kernel(tc, xT, w, b, offs, pos1, out):
         def words_of(first, end):
             return pos1_sb[:, first // LIST_ROWS : end // LIST_ROWS]
 
-        def quantize(codes, scales, grouped, first, end):
-            nc.vector.quantize_mx(
-                out=codes[:, first:end].bitcast(FP8X4),
-                scales=scales[:, first:end],
-                in_=grouped[:, first:end, :].rearrange("p n t -> p (n t)"),
-            )
+        def x_grouped(first, end):
+            return x_head[:] if first == 0 else x_rest[:, first - P : end - P, :]
 
-        nc.scalar.activation(w_grouped[:, 0:last, 0], w012[:].indirect(words_of(0, last)), COPY)
-        nc.scalar.activation(w_work[:, 0:P], w012[:].indirect(words_of(last, V)), COPY)
+        def quantize(codes, scales, grouped):
+            nc.vector.quantize_mx(out=codes.bitcast(FP8X4), scales=scales, in_=grouped.rearrange("p n t -> p (n t)"))
+
+        def quantize_words(first, end):
+            quantize(w_codes[:, first:end], w_scales[:, first:end], w_grouped[:, first:end, :])
+
+        nc.scalar.activation(w_grouped[:, P:V, 1], w012[:].indirect(words_of(P, V)), COPY)
+        nc.scalar.activation(staged[:, 1, :], w012[:].indirect(words_of(0, P)), COPY)
         nc.vector.tensor_copy(w_grouped[:, :, 2], w012[:, N : 2 * N].indirect(pos1_sb[:]))
         nc.vector.tensor_copy(w_grouped[:, :, 3], w012[:, 2 * N : 3 * N].indirect(pos1_sb[:]))
 
         def shared_row(place, tile):
-            nc.scalar.activation(x_grouped[:, 0:HALF, place], tile[:].indirect(tokens_of(0, HALF)), COPY)
-            nc.vector.tensor_copy(x_grouped[:, HALF:S, place], tile[:, 0:T].indirect(tokens_of(HALF, S)))
+            nc.vector.tensor_copy(x_grouped(HALF, S)[:, :, place], tile[:, 0:T].indirect(tokens_of(HALF, S)))
+            for first in (0, P):
+                nc.scalar.activation(x_grouped(first, first + P)[:, :, place], tile[:].indirect(tokens_of(first, first + P)), COPY)
 
         nc.vector.tensor_copy(x1_picked[:], x01[:, T : 2 * T].indirect(tokens_of(0, HALF)))
-        shared_row(0, x01)
-        nc.vector.tensor_copy(x_grouped[:, HALF:S, 2], x01[:, T : 2 * T].indirect(tokens_of(HALF, S)))
-        nc.scalar.copy(x_grouped[:, 0:HALF, 2], x1_picked[:])
+        shared_row(1, x01)
+        nc.vector.tensor_copy(x_grouped(HALF, S)[:, :, 2], x01[:, T : 2 * T].indirect(tokens_of(HALF, S)))
+        for first in (0, P):
+            nc.scalar.copy(x_grouped(first, first + P)[:, :, 2], x1_picked[:, first : first + P])
         shared_row(3, x2)
-        shared_row(1, x3)
-        quantize(x_codes, x_scales, x_grouped, HALF, S)
-        quantize(x_codes, x_scales, x_grouped, 0, HALF)
+        shared_row(0, x3)
+        x_scales = [sb("x_scales0", [P, HALF], U8), reuse.tile([P, HALF], U8, name="x_scales1", align_bytes=ALIGN, offset=0)]
+        for first in (0, P):
+            quantize(x_codes[:, first : first + P], x_scales[0][:, first : first + P], x_grouped(first, first + P))
+        quantize(x_codes[:, HALF:S], x_scales[1][:], x_grouped(HALF, S))
 
-        for first in range(0, last, P):
-            nc.scalar.activation(w_grouped[:, first : first + P, 1], w3[:].indirect(words_of(first, first + P)), COPY)
-        quantize(w_codes, w_scales, w_grouped, 0, P)
-        nc.vector.tensor_copy(w_work[:, P : 2 * P], w3[:].indirect(words_of(last, V)))
-        quantize(w_codes, w_scales, w_grouped, P, 2 * P)
-        nc.vector.tensor_copy(w_grouped[:, last:V, 0:2], w_work[:, 0 : 2 * P].rearrange("p (r n) -> p n r", r=2))
-        quantize(w_codes, w_scales, w_grouped, 2 * P, last)
-        quantize(w_codes, w_scales, w_grouped, last, V)
+        for first, end in ((last, V - EDGE), (V - EDGE, V), (2 * P, last), (P, 2 * P)):
+            nc.scalar.activation(w_grouped[:, first:end, 0], w3[:].indirect(words_of(first, end)), COPY)
+        quantize_words(last, V - EDGE)
+        quantize_words(V - EDGE, V)
+        quantize_words(2 * P, last)
+        for first in (0, EDGE):
+            nc.vector.tensor_copy(staged[:, 0, first : first + EDGE], w3[:].indirect(words_of(first, first + EDGE)))
+        quantize_words(P, 2 * P)
+        for first in (0, EDGE):
+            nc.vector.tensor_copy(w_grouped[:, first : first + EDGE, 0:2], staged[:, :, first : first + EDGE].rearrange("p r n -> p n r"))
+        for first in (0, EDGE):
+            quantize_words(first, first + EDGE)
 
-        for m in range(W_TILES):
-            words = slice(m * P, (m + 1) * P)
-            res = sb(f"res{m}", [P, S], F32)
-            for first in range(0, S, HALF):
-                tokens = slice(first, first + HALF)
-                acc = psum.tile([P, HALF], F32, name=f"acc{(m * S + first) // HALF}")
-                nc.tensor.matmul_mx(
-                    out=acc[:],
-                    lhsT=w_codes[:, words].bitcast(FP8X4),
-                    lhsT_scale=w_scales[:, words],
-                    rhs=x_codes[:, tokens].bitcast(FP8X4),
-                    rhs_scale=x_scales[:, tokens],
-                    start=True,
-                    stop=True,
-                )
-                nc.scalar.activation(res[:, tokens], acc[:], GELU, bias=b_cols[:, m * QUADRANT : m * QUADRANT + 1])
-                nc.sync.dma_start(out[words, tokens], res[:, tokens])
+        res = [sb(f"res{m}", [P, S], F32) for m in range(W_TILES)]
+        pieces = [(m, first, first + HALF) for m in reversed(range(W_TILES)) for first in range(0, S, HALF)]
+        pieces = [(W_TILES - 1, 0, P), (W_TILES - 1, P, HALF)] + pieces[1:]
+        for i, (m, first, end) in enumerate(pieces):
+            words, tokens = slice(m * P, (m + 1) * P), slice(first, end)
+            acc = psum.tile([P, HALF], F32, name=f"acc{i % BANKS}")
+            nc.tensor.matmul_mx(
+                out=acc[:, 0 : end - first],
+                lhsT=w_codes[:, words].bitcast(FP8X4),
+                lhsT_scale=w_scales[:, words],
+                rhs=x_codes[:, tokens].bitcast(FP8X4),
+                rhs_scale=x_scales[first // HALF][:, first % HALF : first % HALF + end - first],
+                start=True,
+                stop=True,
+            )
+            nc.scalar.activation(res[m][:, tokens], acc[:, 0 : end - first], GELU, bias=b_cols[:, m * QUADRANT : m * QUADRANT + 1])
+            if end % HALF == 0:
+                nc.sync.dma_start(out[words, end - HALF : end], res[m][:, end - HALF : end])

@@ -20,6 +20,7 @@ LIST_ROWS = 16
 W_TILES = V // P
 HALF = S // 2
 QUADRANT = 32
+BIAS_ROW = QUADRANT - 1
 ALIGN = 256
 BANKS = 8
 EDGE = 64
@@ -43,14 +44,15 @@ def tile_picked_cross_gelu_l_kernel(tc, xT, w, b, offs, pos1, out):
         w012, w3 = sb("w012", [P, 3 * N], F32), sb("w3", [P, N], F32)
         x01, x2, x3 = sb("x01", [P, 2 * T], F32), sb("x2", [P, T], F32), sb("x3", [P, T], F32)
         b_rows, b_cols = sb("b_rows", [P, P], F32), sb("b_cols", [P, P], F32)
-        nc.gpsimd.memset(b_rows[:], 0.0)
+        for first in range(0, P, QUADRANT):
+            nc.gpsimd.memset(b_rows[first : first + BIAS_ROW, :], 0.0)
         nc.scalar.dma_start(w012[:], w_rows[:, 0 : 3 * N])
-        nc.scalar.dma_start(
-            b_rows[0:P:QUADRANT, :].rearrange("q (m j) -> q m j", j=QUADRANT),
-            b.rearrange("(m q j) o -> q m (j o)", m=W_TILES, j=QUADRANT),
-        )
         nc.sync.dma_start(pos1_sb[:], pos1)
         nc.sync.dma_start(offs_sb[:], offs)
+        nc.sync.dma_start(
+            b_rows[BIAS_ROW:P:QUADRANT, :].rearrange("q (m j) -> q m j", j=QUADRANT),
+            b.rearrange("(m q j) o -> q m (j o)", m=W_TILES, j=QUADRANT),
+        )
         nc.sync.dma_start(x01[:], x_rows[:, 0 : 2 * T])
         nc.sync.dma_start(x2[:], x_rows[:, 2 * T : 3 * T])
         nc.sync.dma_start(x3[:], x_rows[:, 3 * T : 4 * T])
@@ -137,6 +139,6 @@ def tile_picked_cross_gelu_l_kernel(tc, xT, w, b, offs, pos1, out):
                 start=True,
                 stop=True,
             )
-            nc.scalar.activation(res[m][:, tokens], acc[:, 0 : end - first], GELU, bias=b_cols[:, m * QUADRANT : m * QUADRANT + 1])
+            nc.scalar.activation(res[m][:, tokens], acc[:, 0 : end - first], GELU, bias=b_cols[:, m * QUADRANT + BIAS_ROW : (m + 1) * QUADRANT])
             if end % HALF == 0:
                 nc.sync.dma_start(out[words, end - HALF : end], res[m][:, end - HALF : end])

from contextlib import ExitStack

import concourse.mybir as mybir

K, T, S, V, N = 512, 2048, 512, 512, 1024
FLOPS = 2 * K * S * V

F32 = mybir.dt.float32
BF16 = mybir.dt.bfloat16
U32 = mybir.dt.uint32
U16 = mybir.dt.uint16
U8 = mybir.dt.uint8
FP8X4 = mybir.dt.float8_e4m3fn_x4
GELU = mybir.ActivationFunctionType.Gelu_apprx_tanh
COPY = mybir.ActivationFunctionType.Copy

P = 128
PACK = 4
LIST_ROWS = 16
W_TILES = V // P
HALF = S // 2
QUADRANT = 32
BIAS_ROW = QUADRANT - 1
ALIGN = 256
BANKS = 8
EDGE = 64


def tile_picked_cross_gelu_l_kernel(tc, xT, w, b, offs, pos1, out):
    nc = tc.nc
    x_rows = xT.rearrange("(p r) c -> p (r c)", r=PACK)
    w_rows = w.rearrange("(p r) c -> p (r c)", r=PACK)

    with ExitStack() as ctx:
        keep = ctx.enter_context(tc.tile_pool(name="keep", bufs=1))
        reuse = ctx.enter_context(tc.tile_pool(name="reuse", bufs=1))
        psum = ctx.enter_context(tc.psum_pool(name="psum", bufs=1))

        def sb(name, shape, dtype):
            return keep.tile(shape, dtype, name=name, align_bytes=ALIGN)

        pos1_sb = sb("pos1_sb", [P, V // LIST_ROWS], U16)
        offs_sb = sb("offs_sb", [P, S // LIST_ROWS], U16)
        w012, w3 = sb("w012", [P, 3 * N], F32), sb("w3", [P, N], F32)
        x01, x2, x3 = sb("x01", [P, 2 * T], F32), sb("x2", [P, T], F32), sb("x3", [P, T], F32)
        b_rows, b_cols = sb("b_rows", [P, P], F32), sb("b_cols", [P, P], F32)
        for first in range(0, P, QUADRANT):
            nc.gpsimd.memset(b_rows[first : first + BIAS_ROW, :], 0.0)
        nc.scalar.dma_start(w012[:], w_rows[:, 0 : 3 * N])
        nc.sync.dma_start(pos1_sb[:], pos1)
        nc.sync.dma_start(offs_sb[:], offs)
        nc.sync.dma_start(
            b_rows[BIAS_ROW:P:QUADRANT, :].rearrange("q (m j) -> q m j", j=QUADRANT),
            b.rearrange("(m q j) o -> q m (j o)", m=W_TILES, j=QUADRANT),
        )
        nc.sync.dma_start(x01[:], x_rows[:, 0 : 2 * T])
        nc.sync.dma_start(x2[:], x_rows[:, 2 * T : 3 * T])
        nc.sync.dma_start(x3[:], x_rows[:, 3 * T : 4 * T])
        nc.sync.dma_start(w3[:], w_rows[:, 3 * N : 4 * N])
        nc.vector.transpose(b_cols[:], b_rows[:])

        warm = keep.tile([P, 8], F32, name="warm")
        nc.vector.memset(warm[:], 0.0)
        warm_out = keep.tile([P, 8], F32, name="warm_out")
        nc.scalar.activation(warm_out[:], warm[:], GELU)

        w_codes, w_scales = sb("w_codes", [P, V], U32), sb("w_scales", [P, V], U8)
        x_codes = sb("x_codes", [P, S], U32)
        w_work = sb("w_work", [P, V * PACK + 2 * P], BF16)
        w_grouped = w_work[:, 0 : V * PACK].rearrange("p (n t) -> p n t", t=PACK)
        staged = w_work[:, V * PACK - P : V * PACK - P + 2 * P].rearrange("p (r n) -> p r n", r=2)
        x_head = reuse.tile([P, P, PACK], BF16, name="x_head", align_bytes=ALIGN, offset=0)
        x_rest = sb("x_rest", [P, S - P, PACK], BF16)
        x1_picked = sb("x1_picked", [P, HALF], F32)
        last = V - P

        def tokens_of(first, end):
            return offs_sb[:, first // LIST_ROWS : end // LIST_ROWS]

        def words_of(first, end):
            return pos1_sb[:, first // LIST_ROWS : end // LIST_ROWS]

        def x_grouped(first, end):
            return x_head[:] if first == 0 else x_rest[:, first - P : end - P, :]

        def quantize(codes, scales, grouped):
            nc.vector.quantize_mx(out=codes.bitcast(FP8X4), scales=scales, in_=grouped.rearrange("p n t -> p (n t)"))

        def quantize_words(first, end):
            quantize(w_codes[:, first:end], w_scales[:, first:end], w_grouped[:, first:end, :])

        nc.scalar.activation(w_grouped[:, P:V, 1], w012[:].indirect(words_of(P, V)), COPY)
        nc.scalar.activation(staged[:, 1, :], w012[:].indirect(words_of(0, P)), COPY)
        nc.vector.tensor_copy(w_grouped[:, :, 2], w012[:, N : 2 * N].indirect(pos1_sb[:]))
        nc.vector.tensor_copy(w_grouped[:, :, 3], w012[:, 2 * N : 3 * N].indirect(pos1_sb[:]))

        def shared_row(place, tile):
            nc.vector.tensor_copy(x_grouped(HALF, S)[:, :, place], tile[:, 0:T].indirect(tokens_of(HALF, S)))
            for first in (0, P):
                nc.scalar.activation(x_grouped(first, first + P)[:, :, place], tile[:].indirect(tokens_of(first, first + P)), COPY)

        nc.vector.tensor_copy(x1_picked[:], x01[:, T : 2 * T].indirect(tokens_of(0, HALF)))
        shared_row(1, x01)
        nc.vector.tensor_copy(x_grouped(HALF, S)[:, :, 2], x01[:, T : 2 * T].indirect(tokens_of(HALF, S)))
        for first in (0, P):
            nc.scalar.copy(x_grouped(first, first + P)[:, :, 2], x1_picked[:, first : first + P])
        shared_row(3, x2)
        shared_row(0, x3)
        x_scales = [sb("x_scales0", [P, HALF], U8), reuse.tile([P, HALF], U8, name="x_scales1", align_bytes=ALIGN, offset=0)]
        for first in (0, P):
            quantize(x_codes[:, first : first + P], x_scales[0][:, first : first + P], x_grouped(first, first + P))
        quantize(x_codes[:, HALF:S], x_scales[1][:], x_grouped(HALF, S))

        for first, end in ((last, V - EDGE), (V - EDGE, V), (2 * P, last), (P, 2 * P)):
            nc.scalar.activation(w_grouped[:, first:end, 0], w3[:].indirect(words_of(first, end)), COPY)
        quantize_words(last, V - EDGE)
        quantize_words(V - EDGE, V)
        quantize_words(2 * P, last)
        for first in (0, EDGE):
            nc.vector.tensor_copy(staged[:, 0, first : first + EDGE], w3[:].indirect(words_of(first, first + EDGE)))
        quantize_words(P, 2 * P)
        for first in (0, EDGE):
            nc.vector.tensor_copy(w_grouped[:, first : first + EDGE, 0:2], staged[:, :, first : first + EDGE].rearrange("p r n -> p n r"))
        for first in (0, EDGE):
            quantize_words(first, first + EDGE)

        res = [sb(f"res{m}", [P, S], F32) for m in range(W_TILES)]
        pieces = [(m, first, first + HALF) for m in reversed(range(W_TILES)) for first in range(0, S, HALF)]
        pieces = [(W_TILES - 1, 0, P), (W_TILES - 1, P, HALF)] + pieces[1:]
        for i, (m, first, end) in enumerate(pieces):
            words, tokens = slice(m * P, (m + 1) * P), slice(first, end)
            acc = psum.tile([P, HALF], F32, name=f"acc{i % BANKS}")
            nc.tensor.matmul_mx(
                out=acc[:, 0 : end - first],
                lhsT=w_codes[:, words].bitcast(FP8X4),
                lhsT_scale=w_scales[:, words],
                rhs=x_codes[:, tokens].bitcast(FP8X4),
                rhs_scale=x_scales[first // HALF][:, first % HALF : first % HALF + end - first],
                start=True,
                stop=True,
            )
            nc.scalar.activation(res[m][:, tokens], acc[:, 0 : end - first], GELU, bias=b_cols[:, m * QUADRANT + BIAS_ROW : (m + 1) * QUADRANT])
            if end % HALF == 0:
                nc.sync.dma_start(out[words, end - HALF : end], res[m][:, end - HALF : end])
